import numpy as np, ml_dtypes
CORES = [2,3,42,43,82,83,122,123]
N = 8
import mx_ref
BF = ml_dtypes.bfloat16
def cut(t, i, w=512):
    return t[:, w * i:w * i + w]
def tile(rs):
    return np.stack(rs, axis=2).reshape(128, -1).astype(BF)
def pick(q, e):
    c = np.concatenate([q[0].reshape(128, -1, 4), np.zeros((128, 1, 4), np.uint8)], axis=1); s = np.concatenate([q[1], np.ones((16, 1), np.uint8)], axis=1)
    return (np.ascontiguousarray(c[:, e].reshape(128, -1)), np.ascontiguousarray(s[:, e]))
def join(*qs):
    return (np.concatenate([q[0] for q in qs], axis=1), np.concatenate([q[1] for q in qs], axis=1))
def put(q, e, v):
    c, s = q[0].reshape(128, -1, 4).copy(), q[1].copy(); c[:, e] = v[0].reshape(128, -1, 4); s[:, e] = v[1]
    return (c.reshape(128, -1), s)
def pk(c, s):
    return (np.ascontiguousarray(c), mx_ref.live(s))
def emit(q):
    return q[0], q[1]
def f(rng, *shape):
    return mx_ref.flush((rng.standard_normal(shape, dtype=np.float32) * np.exp2(rng.integers(-2, 3, shape[:-1] + (1,)))).astype(BF))
def wide(rng, *shape, cols=0):
    v = rng.standard_normal(shape, dtype=np.float32) * np.exp2(rng.integers(-12, 13, shape)).astype(np.float32)
    if cols: v *= np.repeat(np.exp2(rng.integers(-cols, cols + 1, shape[:-2] + (1, shape[-1] // 4))) * (rng.random(shape[:-2] + (1, shape[-1] // 4)) > 0.0625), 4, axis=-1).astype(np.float32)
    return mx_ref.flush(v.astype(BF))
P, S, R = 256, 32, 3
E = P + 2 * S * R
def randoms(rng):
    s = np.where(rng.random((N, P)) < rng.random((N, 1)), -1, 1)
    x = np.abs(f(rng, N, 128, 4 * P).astype(np.float32)) * np.repeat(s, 4, axis=1)[:, None, :].astype(np.float32)
    a = f(rng, N, 128, 512).astype(np.float32) + np.float32(0.05) * rng.standard_normal((N, 1, 1)).astype(np.float32)
    return {"x": mx_ref.flush(x.astype(BF)), "a": mx_ref.flush(a.astype(BF)), "w": f(rng, N, 128, 2048)}
def planted(rng, n, sign):
    up = np.stack([rng.permutation(128) < n[r] for r in range(N)])
    a = (1 + rng.random((N, 128, 512))) * np.exp2(rng.integers(-2, 3, (N, 128, 1))) * np.repeat(np.where(up, 1.0, -1.0), 4, axis=1)[:, None, :]
    x = np.abs(f(rng, N, 128, 4 * P).astype(np.float32)) * np.float32(sign)
    return {"x": x.astype(BF), "a": a.astype(np.float32).astype(BF), "w": f(rng, N, 128, 2048)}
def setup_inputs(rng):
    return randoms(rng)
def setup_inputs_shrink(rng):
    k = N // 2 - int(rng.integers(0, 2))
    n = rng.integers(0, 2, N)
    n[k] = rng.integers(112, 128)
    d = planted(rng, n, 1)
    d["x"][k, :, :4 * S * R] = 0
    d["x"][k, :, 4 * (P - S * R):] = 0
    return d
def setup_inputs_grow(rng):
    k, big = N // 2 - int(rng.integers(0, 2)), int(rng.integers(113, 129))
    less = big if N > 4 else 3 * big // 4
    n = np.full(N, less - 1)
    if k < N // 2: n[:k] = big - 1
    else: n[k + 1:] = big - 1
    n[k] = rng.integers(0, 4)
    return planted(rng, n, 1)
def setup_inputs_spread(rng):
    return {**randoms(rng), "x": wide(rng, N, 128, 4 * P, cols=6)}
def setup_inputs_part(rng):
    k, m = (N - 1) * int(rng.integers(0, 2)), 4 * int(rng.integers(0, 4)) + 2
    d = planted(rng, np.where(np.arange(N) == k, 1, 0), 1)
    on = np.zeros(P, bool)
    on[16 + rng.permutation(P - 32)[:m]] = True
    d["x"][k][:, np.repeat(~on, 4)] = 0
    return d
def setup_inputs_turn(rng):
    k = N // 2 - int(rng.integers(0, 2))
    n = np.full(N, int(rng.integers(112, 128)))
    n[k] = rng.integers(0, 4)
    return planted(rng, n, -1)
def check_inputs(d):
    b = []
    for k in ("x", "a", "w"):
        v = np.abs(d[k].astype(np.float32))
        if not (np.isfinite(v).all() and ((v == 0) | (v >= 2.0 ** -30) & (v <= 2.0 ** 30)).all()): b.append("a value of " + k)
    return b
def held(row, bo, r, m=4):
    e = np.arange(bo[r], bo[r + 1])
    return pick(row, np.concatenate([e, np.full(-e.size % m, -1)]))
def moved(bo, cost):
    before, new = np.concatenate([[0], np.cumsum(cost)]), bo.copy()
    for b in range(1, N):
        g = int(np.argmax(N * before >= b * before[-1]))
        new[b] = bo[b] + min(S, max(-S, g - int(bo[b])))
    return new
def reference(x, a, w):
    qa = [mx_ref.quantize(np.ascontiguousarray(a[r])) for r in range(N)]
    qw = [[mx_ref.quantize(np.ascontiguousarray(cut(w[r], b))) for b in range(4)] for r in range(N)]
    bo, out = P * np.arange(N + 1), []
    row = join(*[mx_ref.quantize(np.ascontiguousarray(x[r])) for r in range(N)])
    for t in range(R):
        cost = []
        for r in range(N):
            z = mx_ref.matmul(qa[r], held(row, bo, r))[:, :bo[r + 1] - bo[r]]
            cost.append(1 + np.sum(z > 0, axis=0).astype(np.int64))
        bo = moved(bo, np.concatenate(cost))
        new = []
        for r in range(N):
            h = held(row, bo, r)
            v = tile([np.maximum(mx_ref.matmul(qw[r][b], h), np.float32(0)) * np.float32(0.0625) for b in range(4)])
            new.append(pick(mx_ref.quantize(np.ascontiguousarray(v)), np.arange(bo[r + 1] - bo[r])))
        row = join(*new)
        out.append(bo)
    y, oc, osc = np.zeros((N, 128, E), np.float32), np.zeros((N, 128, 4 * E), np.uint8), np.zeros((N, 16, E), np.uint8)
    for r in range(N):
        n = int(bo[r + 1] - bo[r])
        y[r, :, :n] = mx_ref.matmul(qa[r], held(row, bo, r))[:, :n]
        oc[r], osc[r] = emit(held(row, bo, r, E))
    return {"y": y, "oc": oc, "osc": osc, "bd": np.stack([np.stack(out).astype(np.float32) for r in range(N)])}

@@ -1,0 +1,518 @@
+from concourse.bass import DstId, RemoteDMATransfer
+from concourse.mybir import dt, AluOpType, AxisListType, ActivationFunctionType
+
+N, P, S, R = 8, 256, 32, 3
+E = P + 2 * S * R
+C4, U8, F32, BF, I32, U16 = "float8_e4m3fn_x4", "uint8", "float32", "bfloat16", "int32", "uint16"
+
+
+def _pair(name, n):
+    return {name: ("sbuf", [128, n], C4), name + "s": ("sbuf", [128, n], U8)}
+
+
+SCRATCH = {
+    "hx": ("sbuf", [128, 1024], BF), "ha": ("sbuf", [128, 512], BF), "hw": ("sbuf", [128, 2048], BF),
+    "h1": ("sbuf", [128, 1536], BF), "h2": ("sbuf", [128, 1536], BF), "h3": ("sbuf", [128, 1800], BF),
+    **_pair("xq", 320), **_pair("aq", 128), **_pair("wq", 512), **_pair("v1", 384), **_pair("v2", 384), **_pair("v3", 450),
+    **_pair("ld1", 192), **_pair("ld2", 320), **_pair("p1", 192), **_pair("p2", 192), **_pair("fin", E),
+    "pe": ("psum", [128, 2048], F32), "pl": ("psum", [128, 2048], F32),
+    "junk": ("sbuf", [128, 1280], BF),
+    "land0": ("sbuf", [128, 32], F32), "land1": ("sbuf", [128, 32], F32), "land2": ("sbuf", [128, 32], F32),
+    "ysb": ("sbuf", [128, 450], F32), "yo": ("sbuf", [128, E], F32),
+    "ci": ("sbuf", [128, 4], I32), "ri": ("sbuf", [128, 4], I32), "k": ("sbuf", [128, 64], F32),
+    "it": ("sbuf", [128, 128], F32), "brow": ("sbuf", [128, 36], F32), "dd": ("sbuf", [128, 32], F32),
+    "a16": ("sbuf", [128, 28], F32), "jj": ("sbuf", [128, 28], F32), "jm": ("sbuf", [128, 28], F32),
+    "zero": ("sbuf", [128, 32], F32), "neg": ("sbuf", [128, 28], F32), "sel": ("sbuf", [128, 160], F32), "mx": ("sbuf", [128, 96], F32),
+    "cw": ("sbuf", [128, 128 * 16], F32),
+    "msk": ("sbuf", [128, 128 * 12], F32),
+    "lt": ("sbuf", [128, 128 * 3], F32), "sm": ("sbuf", [128, 128 * 3], F32), "uu": ("sbuf", [128, 132 * 3], F32),
+    "vv": ("sbuf", [128, 128 * 3], F32), "cmp": ("sbuf", [128, 128 * 3], F32),
+    "xx": ("sbuf", [128, 64 * 3], F32), "yy": ("sbuf", [128, 96 * 3], F32), "yt": ("sbuf", [128, 96 * 3], F32),
+    "cn": ("sbuf", [128, 32], F32), "bh": ("sbuf", [128, 32], F32), "bt": ("sbuf", [128, 32], F32), "bo": ("sbuf", [128, 16], F32),
+    "of1": ("sbuf", [128, 4], U16), "of2": ("sbuf", [128, 4], U16), "of3": ("sbuf", [128, 28], U16),
+    "t2": ("sbuf", [128, 8], F32), "d0": ("sbuf", [128, 196], F32), "d1": ("sbuf", [128, 196], F32), "sc": ("sbuf", [128, 196], F32),
+}
+POOL = {"v": 56, "s": 40, "t": 22, "g": 4, "d": 16}
+SEMAPHORES = [q + str(i) for q in POOL for i in range(POOL[q])] + ["ex", "e1", "e2", "ga0", "ga1", "ga2", "sent"]
+
+A = AluOpType
+ACT = ActivationFunctionType
+FAR = 65536.0
+BIG = 2097152.0
+TINY = 2.0 ** -120
+
+
+def rank_program(g, core, T, topo):
+    r = T.rank_of(core)
+    if r is None:
+        return
+    cores = T.cores
+    left = cores[r - 1] if r > 0 else None
+    right = cores[r + 1] if r < N - 1 else None
+    V, SC, PE, SY = g.vector, g.scalar, g.tensor, g.sync
+    Q = {"v": V, "s": SC, "t": PE, "g": g, "y": SY}
+    ID = ACT.Identity
+
+    total, seen, nxt = {}, {q: {} for q in Q}, {q: 0 for q in POOL}
+
+    def wait(q, *evs):
+        for ev in evs:
+            if ev is not None and seen[q].get(ev[0], 0) < ev[1]:
+                Q[q].wait_ge(T.sem[ev[0]], ev[1])
+                seen[q][ev[0]] = ev[1]
+
+    def group(q, calls, pool=None, inc=1):
+        pool = pool or q
+        name = pool + str(nxt[pool] % POOL[pool])
+        nxt[pool] += 1
+        if total.get(name, 0):
+            wait(q, (name, total[name]))
+        for c in calls:
+            c().then_inc(T.sem[name], inc)
+            total[name] = total.get(name, 0) + inc
+        return (name, total[name])
+
+    def dma(q, pairs):
+        return group(q, [(lambda o=o, i=i: Q[q].dma_start(o, i)) for o, i in pairs], pool="d", inc=16)
+
+    def ts(out, in0, s1, op0, s2=None, op1=None):
+        if op1 is None:
+            return lambda: V.tensor_scalar(out, in0, s1, None, op0)
+        return lambda: V.tensor_scalar(out, in0, s1, s2, op0, op1)
+
+    def tt(out, a, b, op):
+        return lambda: V.tensor_tensor(out, a, b, op)
+
+    def cp(out, a):
+        return lambda: V.tensor_copy(out, a)
+
+    def ms(out, c):
+        return lambda: V.memset(out, c)
+
+    def red(out, a):
+        return lambda: V.tensor_reduce(out, a, AxisListType.X, A.add)
+
+    def tr(out, a):
+        return lambda: V.transpose(out, a)
+
+    def act(out, a, f, bias=0.0, scale=1.0):
+        if f == ACT.Copy:
+            return lambda: SC.activation(out, a, f)
+        return lambda: SC.activation(out, a, f, bias=bias, scale=scale)
+
+    def qz(q, lo, hi, tile, at=None):
+        at = lo if at is None else at
+        return lambda: V.quantize_mx(T[q][:, lo:hi], T[q + "s"][:, lo:hi], tile[:, 4 * at:4 * (at + hi - lo)])
+
+    def mm(ps, bank, sq, s0, mq, lo, hi):
+        return lambda: PE.matmul_mx(ps[:, 512 * bank:512 * bank + hi - lo], T[sq][:, s0:s0 + 128], T[sq + "s"][:, s0:s0 + 128],
+                                    T[mq][:, lo:hi], T[mq + "s"][:, lo:hi], True, True)
+
+    def evac(q, tile, b, at, ps, lo, n):
+        o, i = tile[:, 4 * at + b:4 * (at + n):4], ps[:, 512 * b + lo:512 * b + lo + n]
+        return act(o, i, ACT.Relu, scale=0.0625) if q == "s" else ts(o, i, 0.0, A.max, 0.0625, A.mult)
+
+    nj = [0]
+
+    def count(ps, bank, land, j):
+        jk = T.junk[:, 128 * nj[0]:128 * nj[0] + 128]
+        nj[0] += 1
+        return lambda: SC.activation(jk, ps[:, 512 * bank:512 * bank + 128], ACT.Sign, bias=-TINY, scale=1.0,
+                                     accum_out=land[:, 4 * r + j:4 * r + j + 1])
+
+    others = [c for c in cores if c != core]
+    far = [c for c in others if topo.chip(c) != topo.chip(core)]
+    far.sort(key=lambda c: topo.same_plane(topo.chip(c), topo.chip(core)) or topo.mates(topo.chip(c), topo.chip(core)))
+    near = [c for c in others if topo.chip(c) == topo.chip(core)]
+
+    def engines(src, dst):
+        if topo.chip(src) != topo.chip(dst):
+            return topo.engines(src, dst)
+        out = [c for c in cores if topo.chip(c) != topo.chip(src)][0]
+        return [e for e in topo.engines(src, dst) if e not in topo.engines(src, out)]
+
+    sent = [0]
+
+    def xfer(dsts, src, dst, sem):
+        en = engines(core, dsts[0])
+        sent[0] += len(en)
+        return RemoteDMATransfer(dst_ids=[DstId(rid=topo.addr(c)[0], pnc=topo.addr(c)[1]) for c in dsts],
+                                 dma_engine_mask=sum(1 << e for e in en), remote_sem=T.sem[sem], srcs=[src], dsts=[dst for c in dsts])
+
+    def fused(trs):
+        g.remote_dma_fused(trs, local_sem=T.sem.sent)
+
+    def edges(src, dst, moves, sem, split):
+        moves = sorted(moves, key=lambda m: m[0] in near)
+        for plane in (False, True):
+            trs = []
+            for c, a, b, n in moves:
+                if plane:
+                    trs.append(xfer([c], T[src + "s"][:, a:a + n], T[dst + "s"][:, b:b + n], sem))
+                else:
+                    trs.append(xfer([c], T[src][:, a:a + n].bitcast(dt.uint8), T[dst][:, b:b + n].bitcast(dt.uint8), sem))
+            for part in ([[t] for t in trs] if split else [trs]):
+                fused(part)
+
+    def share(land, sem):
+        v = land[:, 4 * r:4 * r + 4]
+        fused([xfer(far, v, v, sem), xfer(near, v, v, sem)])
+
+    n_edge = sum(2 * len(engines(c, core)) for c in (left, right) if c is not None)
+    n_all = sum(len(engines(c, core)) for c in others)
+    EX, E1, E2 = ("ex", n_edge), ("e1", n_edge), ("e2", n_edge)
+    GA = [("ga%d" % t, n_all) for t in range(R)]
+    lands = [T.land0, T.land1, T.land2]
+
+    def K(i, p=32):
+        return T.k[0:p, i:i + 1]
+    RHO, INN, BB, PM, CC, SIG, R127, LIM1, LIMP, LIMA, I0, AB, CS, COL0, SIGM, KK, K1, K2, K0, I130 = range(20)
+    COLM, NB = 20, 24
+    TH2, TH3, TH4, TH5, KU, VV_, CL64, KR, K224, RR, NT5, EE = range(30, 42)
+
+    def W(i):
+        return T.cw[0:32, 128 * i:128 * i + 128]
+    TP_, G1R, G2S, G0, INV1, INVP, ABT, INV2, G1, G2A, TPP, B2, BQ, A2, G2, TM = range(16)
+
+    def M(t, i):
+        return T.msk[0:32, 128 * (4 * t + i):128 * (4 * t + i) + 128]
+
+    def CN(i, p=128):
+        return T.cn[0:p, i:i + 1]
+
+    LX = dma("y", [(T.hx[:], T.x[:])])
+    LA = dma("y", [(T.ha[:], T.a[:])])
+    LW = [dma("y", [(T.hw[:, 512 * b:512 * b + 512], T.w[:, 512 * b:512 * b + 512])]) for b in range(4)]
+
+    io = lambda o, p, b, c: (lambda: g.iota(o, p, b, c, allow_small_or_imprecise_dtypes=True))
+    G1e = group("g", [lambda: g.iota(T.ci[:], [[1, 4]], 0, 1)])
+    G2e = group("g", [io(T.brow[0:32, :], [[1, 9], [0, 4]], 0, 0), io(T.dd[0:32, :], [[1, 32]], 0, -1), io(T.a16[:], [[16, 28]], 0, 0)])
+    G3e = group("g", [io(T.it[0:32, :], [[1, 128]], 0, 0)])
+
+    fills = [ms(T.zero[:], 0.0), ms(T.neg[:], -1.0), ms(T.land0[:, 4 * r:4 * r + 4], 0.0), ms(T.h1[:, 0:128], 0.0), ms(T.h1[:, 1408:1536], 0.0),
+             ms(T.bh[0:32, :], 0.0), ms(T.bo[0:32, :], float(N * P)), ms(T.uu[0:32, 0:396:132], 0.0), ms(T.h3[:, 0:8], 0.0),
+             ms(T.d0[:, 0:196:7], 0.0), ms(T.d1[:, 6:196:7], 0.0), ms(T.d1[:, 2:196:7], -384.0)]
+    if left is None:
+        fills += [ms(T.cn[:, 0:6:2], float(S)), ms(T.h1[:, 4 * 192:4 * 224], 0.0)]
+    if right is None:
+        fills += [ms(T.cn[:, 1:6:2], float(S)), ms(T.h1[:, 4 * 160:4 * 192], 0.0)]
+    FILL = group("v", fills)
+    wait("v", G1e)
+    e = group("v", [ts(T.ri[:, 0:2], T.ci[:, 0:2], 1, A.arith_shift_right, 1, A.bitwise_and),
+                    ts(T.ri[:, 2:3], T.ci[:, 2:3], 2, A.arith_shift_right), ts(T.ri[:, 3:4], T.ci[:, 0:1], 15, A.bitwise_and),
+                    cp(K(CC, 128), T.ci[:, 0:1])])
+    wait("v", e)
+    KF = group("v", [cp(T.k[:, 0:4], T.ri[:])])
+    wait("v", KF, G2e, FILL)
+    brow = T.brow[0:32, 2:34]
+    L3 = group("v", [ts(K(SIG), K(RHO), -2.0, A.mult, 1.0, A.add), ts(K(R127), K(RHO), 127.0, A.mult),
+                     ts(T.jj[:], T.a16[:], K(PM, 128), A.add),
+                     ts(T.sel[0:32, 96:128], T.zero[0:32, :], K(BB), A.add, float(r), A.is_equal),
+                     ts(T.sel[0:32, 128:160], T.zero[0:32, :], K(BB), A.add, float(r + 1), A.is_equal),
+                     ts(T.sel[0:32, 64:96], brow, K(BB), A.is_equal, 0.5, A.mult),
+                     ts(T.mx[0:32, 32:64], T.dd[0:32, :], 0.0, A.is_gt, 16.0, A.mult), ts(T.mx[0:32, 64:96], brow, 16.0 / N, A.mult)])
+    wait("s", KF, e)
+    S1 = group("s", [act(K(AB), K(CC), ACT.Abs, bias=-15.5), act(K(LIM1), K(INN), ID, bias=64.0, scale=32.0),
+                     act(K(LIMP), K(INN), ID, bias=32.0, scale=-32.0), act(K(LIMA), K(INN), ID, bias=16.0, scale=1000.0),
+                     act(K(I0), K(INN), ID, bias=-FAR, scale=FAR), act(K(I130), K(INN), ID, scale=130.0)])
+    wait("s", L3, G3e, S1)
+    S2 = group("s", [act(W(TP_), T.it[0:32, :], ID, bias=K(R127), scale=K(SIG)),
+                     act(M(0, 0), T.it[0:32, :], ID, bias=K(INN), scale=0.0),
+                     act(M(0, 1), T.it[0:32, :], ID, bias=K(I130), scale=0.0),
+                     act(T.sel[0:32, 0:64], T.sel[0:32, 96:160], ID, scale=0.5)])
+
+    def barrier(t, gs, *evs):
+        wait("s", *evs)
+        e = group("s", [act(M(t, 2), gs, ACT.Abs, bias=K(NB + t))])
+        wait("s", e)
+        return group("s", [act(M(t, 3), M(t, 2), ACT.Relu, bias=-16.0 * BIG, scale=BIG)])
+
+    wait("v", LX)
+    XQ = group("v", [qz("xq", 0, 256, T.hx)])
+    wait("g", XQ)
+    lslot = lambda c: 256 if T.rank_of(c) == N - 1 else 288
+    edges("xq", "xq", ([(left, 0, 256, 32)] if left is not None else []) + ([(right, 224, lslot(right), 32)] if right is not None else []), "ex", True)
+    wait("v", LA)
+    AQ = group("v", [qz("aq", 0, 128, T.ha)])
+    wait("t", XQ, AQ)
+    mc = [group("t", [mm(T.pl, j, "xq", 128 * j, "aq", 0, 128)]) for j in range(2)]
+    CS0 = []
+    wait("s", FILL)
+    for j in range(2):
+        wait("s", mc[j])
+        CS0.append(group("s", [count(T.pl, j, T.land0, 1 + j)]))
+    wait("g", FILL, *CS0)
+    share(T.land0, "ga0")
+
+    wait("v", L3, S1)
+    L4 = group("v", [ts(K(CS), K(CC), K(SIG), A.mult, 64.0, A.mult), ts(K(COL0), K(BB), K(SIG), A.mult, float(P), A.mult),
+                     ts(K(SIGM), K(AB), 14.0, A.is_lt, K(SIG), A.mult), tt(T.mx[0:32, 0:32], T.mx[0:32, 64:96], T.mx[0:32, 32:64], A.subtract)])
+    wait("v", L4)
+    L5 = group("v", [ts(K(KK), K(RHO), -64.0, A.mult, K(CS), A.add), ts(K(COLM), K(SIGM), -32.0, A.mult, K(COL0), A.add),
+                     ts(K(NB), K(COL0), -1.0, A.mult, -15.5, A.add), ts(K(EE), K(CC), 0.0, A.is_equal, -1.0, A.mult)])
+    wait("v", L5)
+    L6 = group("v", [ts(K(K1), K(KK), -32.0, A.add), ts(K(K2), K(KK), -64.0, A.add), ts(K(K0), K(KK), -64.0, A.add, K(I0), A.add)])
+    wait("s", S2, L6)
+    S3 = group("s", [act(W(ABT), W(TP_), ACT.Abs, bias=-47.5), act(W(G1R), W(TP_), ID, bias=K(K1)),
+                     act(W(G2S), W(TP_), ID, bias=K(K2)), act(W(G0), W(TP_), ID, bias=K(K0)), act(W(TM), W(TP_), ID, bias=-32.0)])
+    N0 = barrier(0, W(G0), S3, L5)
+
+    gap = [[ts(W(INV1), W(TP_), K(LIM1), A.is_ge, -FAR, A.mult), ts(W(INVP), W(TP_), K(LIMP), A.is_ge, -2 * FAR, A.mult),
+            ts(W(INV2), W(ABT), K(LIMA), A.is_ge, -FAR, A.mult)],
+           [tt(W(G1), W(G1R), W(INV1), A.add), qz("p1", 64, 192, T.hx, 0)],
+           [tt(W(G2A), W(G2S), W(INV2), A.add), qz("p2", 64, 192, T.hx, 0)],
+           [tt(W(TPP), W(TM), W(INVP), A.add)]]
+    WQ, GP = [], []
+    for b in range(4):
+        wait("v", LW[b])
+        WQ.append(group("v", [qz("wq", 128 * b, 128 * b + 128, T.hw)]))
+        if b:
+            wait("v", S3, *GP[:1])
+            GP.append(group("v", gap[b - 1]))
+
+    def early(ps, mq, lo, hi, tile, cuts, evs):
+        out = []
+        for b in range(4):
+            wait("t", evs[b])
+            m = group("t", [mm(ps, b, "wq", 128 * b, mq, lo, hi)])
+            wait("s", m)
+            out.append(group("s", [evac("s", tile, b, at, ps, a, n) for a, at, n in cuts]))
+        return out
+
+    def late(ps, mq, lo, tile, a, at, n):
+        ms_ = [group("t", [mm(ps, b, "wq", 128 * b, mq, lo, lo + 128)]) for b in range(4)]
+        out = []
+        for b in range(4):
+            q = "sv"[b % 2]
+            wait(q, ms_[b])
+            out.append(group(q, [evac(q, tile, b, at, ps, a, n)]))
+        return out
+
+    def costs(ps, banks, vq, land, chunks):
+        ms_ = [group("t", [mm(ps, bk, vq, c0, "aq", 0, 128)]) for bk, (j, c0) in zip(banks, chunks)]
+        out = []
+        for m, bk, (j, c0) in zip(ms_, banks, chunks):
+            wait("s", m)
+            out.append(group("s", [count(ps, bk, land, j)]))
+        return out
+
+    ev = early(T.pe, "xq", 0, 256, T.h1, [(0, 224, 128), (128, 32, 128)], WQ)
+    wait("v", *ev)
+    V1E = group("v", [qz("v1", 0, 128, T.h1), qz("v1", 256, 384, T.h1)])
+    GP.append(group("v", gap[3]))
+    wait("t", EX, *CS0)
+    if left is not None and right is not None:
+        ev = late(T.pl, "xq", 192, T.h1, 64, 160, 64)
+    else:
+        ev = late(T.pl, "xq", 160, T.h1, 96, 160 if left is None else 192, 32)
+    wait("v", *ev)
+    V1L = group("v", [qz("v1", 128, 256, T.h1)])
+    wait("g", V1E, V1L)
+    edges("v1", "ld1", ([(left, 192, 0, 96)] if left is not None else []) + ([(right, 96, 96, 96)] if right is not None else []), "e1", False)
+    wait("t", V1E)
+    CS1 = costs(T.pe, (0, 1), "v1", T.land1, [(1, 256), (2, 0)])
+    wait("t", V1L)
+    CS1 += costs(T.pe, (2, 3), "v1", T.land1, [(0, 192), (3, 64)])
+    wait("g", *CS1)
+    share(T.land1, "ga1")
+
+    def border(t, own, mask, mask130, bar, all_now, hole=None, after=None):
+        lt, sm, vv, cm = (b[0:32, 128 * t:128 * t + 128] for b in (T.lt, T.sm, T.vv, T.cmp))
+        u0, x0, y0 = 132 * t, 64 * t, 96 * t
+        wait("v", GA[t], *own)
+        e = group("v", [tr(T.lt[0:32, 128 * t + 32 * a:128 * t + 32 * a + 32], lands[t][32 * a:32 * a + 32, :]) for a in range(4)])
+        wait("v", e, mask)
+        e = group("v", [tt(sm, lt, M(t, 0), A.mult)])
+        wait("v", e, mask130)
+        e = group("v", [lambda: V.tensor_tensor_scan(T.uu[0:32, u0 + 1:u0 + 129], sm, M(t, 1), 0.0, A.add, A.add)])
+        wait("v", e)
+        e = group("v", [ts(T.xx[0:32, x0:x0 + 32], T.mx[0:32, 0:32], T.uu[0:32, u0 + 128:u0 + 129], A.mult, K(EE), A.add)])
+        wait("v", e)
+        e = group("v", [tr(T.xx[0:32, x0 + 32:x0 + 64], T.xx[0:32, x0:x0 + 32])])
+        wait("v", bar)
+        ev_ = group("v", [tt(vv, T.uu[0:32, u0:u0 + 128], M(t, 3), A.add)])
+        wait("v", e)
+        e = group("v", [red(CN(8 + t, 32), T.xx[0:32, x0 + 32:x0 + 64])])
+        if hole:
+            hole()
+        wait("s", e, ev_)
+        e = group("s", [lambda: SC.activation(cm, vv, ACT.Sign, bias=CN(8 + t, 32), scale=-16.0, accum_out=CN(12 + t, 32))])
+        wait("s", e)
+        e = group("s", [act(T.yy[0:32, y0:y0 + 96], T.sel[0:32, 0:96], ID, bias=8.0, scale=CN(12 + t, 32))])
+        if after:
+            after()
+        wait("v", e)
+        lo, hi = (32 if left is None else 0), (32 if right is None else 64)
+        e = group("v", [tr(T.yt[0:32, y0 + lo:y0 + 96], T.yy[0:32, y0 + lo:y0 + 96])] +
+                  [tr(T.yt[32 * a:32 * a + 32, y0 + lo:y0 + hi], T.yy[0:32, y0 + lo:y0 + hi]) for a in range(1, 4)])
+        wait("v", e)
+        own_ = [red(CN(2 * t + s), T.yt[:, y0 + 32 * s:y0 + 32 * s + 32]) for s in range(2) if (left, right)[s] is not None]
+        rest = [red(CN(16 + t, 32), T.yt[0:32, y0 + 64:y0 + 96])]
+        return group("v", own_ + rest) if all_now else (group("v", own_), rest)
+
+    def columns(t):
+        return group("v", [ts(T.bh[0:32, t:t + 1], CN(16 + t, 32), K(SIGM), A.mult, K(COLM + t), A.add)])
+
+    def masks(t, gs, col, *evs):
+        wait("v", col, *evs)
+        return group("v", [ts(M(t, 0), gs, T.bh[0:32, t - 1:t], A.is_ge)])
+
+    def masks2(t, gs, col, m, *evs):
+        wait("s", col, m)
+        e = group("s", [act(K(NB + t), T.bh[0:32, t - 1:t], ID, bias=-15.5, scale=-1.0), act(M(t, 1), M(t, 0), ID, scale=130.0)])
+        return e, barrier(t, gs, e, *evs)
+
+    def pick(dst, src, n, off):
+        c = group("v", [cp(T[dst][:, 0:64].bitcast(dt.uint32), T[src][:, 0:n].bitcast(dt.uint32).indirect(off[:, 0:4]))])
+        s = group("s", [act(T[dst + "s"][:, 0:64], T[src + "s"][:, 0:n].indirect(off[:, 0:4]), ACT.Copy)])
+        return c, s
+
+    box = {}
+
+    ev = early(T.pl, "v1", 32, 352, T.h2, [(0, 0, 160), (160, 224, 160)], [None] * 4)
+    wait("v", *GP)
+
+    def hole1():
+        wait("v", *ev)
+        box["V2E"] = group("v", [qz("v2", 0, 128, T.h2), qz("v2", 256, 384, T.h2)])
+
+    def after1():
+        wait("t", box["V2E"])
+        box["CS2"] = costs(T.pl, (0, 1), "v2", T.land2, [(1, 256), (2, 0)])
+    B0 = border(0, CS0, S2, None, N0, True, hole1, after1)
+    V2E, CS2 = box["V2E"], box["CS2"]
+    wait("v", B0)
+    j2 = T.jj[:, 0:2]
+    O1 = group("v", [ts(T.of1[:, 0:2], j2, CN(1), A.add) if right is not None else ts(T.of1[:, 0:2], j2, 96.0, A.add),
+                     ts(T.of1[:, 2:4], j2, CN(0), A.add, 96.0, A.add) if left is not None else ts(T.of1[:, 2:4], j2, 0.0, A.add)])
+    COL_0 = columns(0)
+    wait("v", E1, O1)
+    wait("s", E1, O1)
+    pk = pick("p1", "ld1", 192, T.of1)
+    MK1 = masks(1, W(G1), COL_0)
+    wait("t", GP[1], *pk)
+    wait("t", *CS1)
+    ev = late(T.pe, "p1", 0, T.h2, 0, 160, 64)
+    wait("v", *ev)
+    V2L = group("v", [qz("v2", 128, 256, T.h2)])
+    wait("g", V2E, V2L)
+    edges("v2", "ld2", ([(left, 192, 0, 160)] if left is not None else []) + ([(right, 32, 160, 160)] if right is not None else []), "e2", False)
+    wait("t", V2L)
+    CS2 += costs(T.pl, (2, 3), "v2", T.land2, [(0, 192), (3, 64)])
+    wait("g", *CS2)
+    share(T.land2, "ga2")
+
+    M1, N1 = masks2(1, W(G1), COL_0, MK1, GP[1])
+    c0 = T.bh[0:32, 0:1]
+    wait("s", GP[3])
+    BQe = group("s", [act(W(BQ), W(TPP), ID, bias=c0)])
+    ev = early(T.pe, "v2", 0, 384, T.h3, [(0, 2, 384)], [None] * 4)
+    e = group("v", [ts(W(B2), W(G2A), c0, A.is_lt, -FAR, A.mult)])
+    wait("v", e)
+    A2e = group("v", [tt(W(A2), W(G2A), W(B2), A.add)])
+
+    def hole2():
+        wait("v", A2e, BQe)
+        box["G2"] = group("v", [tt(W(G2), W(A2), W(BQ), A.max)])
+        wait("v", *ev)
+        box["V3E"] = group("v", [qz("v3", 0, 322, T.h3)])
+
+    def after2():
+        wait("s", B0, L5)
+        box["C1"] = group("s", [act(K(COLM + 1), K(SIGM), ID, bias=c0, scale=-32.0), act(K(CL64, 128), CN(0), ID, bias=-64.0),
+                                act(K(KR, 128), CN(1), ID, bias=288.0), act(K(K224, 128), CN(0), ID, bias=224.0, scale=-1.0),
+                                act(T.d1[:, 1:196:7], T.neg[:], ID, bias=64.0, scale=CN(1)), act(T.d1[:, 3:196:7], T.neg[:], ID, bias=CN(0), scale=0.0)])
+        wait("s", box["C1"])
+        box["C2"] = group("s", [act(K(KU, 128), CN(0), ID, bias=K(KR, 128), scale=-1.0)])
+    B1 = border(1, CS1, MK1, M1, N1, True, hole2, after2)
+    V3E = box["V3E"]
+    wait("v", B1, box["C1"])
+    e = group("v", [ts(T.t2[:, 0:2], j2, CN(3), A.add, 32.0, A.is_ge), ts(T.t2[:, 2:4], j2, CN(2), A.add, 64.0, A.is_lt)])
+    COL_1 = columns(1)
+    wait("s", B1, box["C2"])
+    C3 = group("s", [act(K(TH2, 128), CN(2), ID, bias=64.0, scale=-1.0), act(K(TH3, 128), CN(2), ID, bias=K(K224, 128), scale=-1.0),
+                     act(K(VV_, 128), CN(2), ID, bias=K(KU, 128), scale=-1.0), act(K(RR, 128), CN(3), ACT.Relu, bias=-32.0),
+                     act(T.d1[:, 0:196:7], T.neg[:], ID, bias=256.0, scale=CN(3))])
+    wait("s", C3)
+    C4e = group("s", [act(K(TH5, 128), CN(3), ID, bias=K(VV_, 128)), act(T.d1[:, 4:196:7], T.neg[:], ID, bias=-192.0, scale=K(TH2, 128))])
+    wait("v", e)
+    e = group("v", [ts(T.t2[:, 4:6], T.t2[:, 0:2], CN(1), A.mult, CN(3), A.add), ts(T.t2[:, 6:8], T.t2[:, 2:4], K(CL64, 128), A.mult, CN(2), A.add)])
+    wait("v", e)
+    o2 = []
+    if right is not None:
+        o2 += [ts(T.of2[:, k:k + 1], T.t2[:, 4 + k:5 + k], K(PM, 128), A.add, 16.0 * k, A.add) for k in range(2)]
+    else:
+        o2 += [ts(T.of2[:, 0:2], j2, 160.0, A.add)]
+    if left is not None:
+        o2 += [ts(T.of2[:, 2 + k:3 + k], T.t2[:, 6 + k:7 + k], K(PM, 128), A.add, 224.0 + 16.0 * k, A.add) for k in range(2)]
+    else:
+        o2 += [ts(T.of2[:, 2:4], j2, 0.0, A.add)]
+    O2 = group("v", o2)
+    MK2 = masks(2, W(G2), COL_1, box["G2"])
+    wait("v", E2, O2)
+    wait("s", E2, O2)
+    pk = pick("p2", "ld2", 320, T.of2)
+    wait("t", GP[2], *pk)
+    wait("t", *CS2)
+    ev = late(T.pl, "p2", 0, T.h3, 0, 386, 64)
+    M2, N2 = masks2(2, W(G2), COL_1, MK2)
+    wait("v", *ev)
+    V3L = group("v", [qz("v3", 322, 450, T.h3)])
+    wait("s", C4e)
+    C5 = group("s", [act(K(TH4, 128), K(RR, 128), ID, bias=K(TH5, 128), scale=-1.0), act(K(NT5, 128), K(TH5, 128), ID, bias=32.0, scale=-1.0),
+                     act(K(COLM + 2), K(SIGM), ID, bias=T.bh[0:32, 1:2], scale=-32.0)])
+    wait("s", C5)
+    ST = group("s", [act(T.jm[:], T.jj[:], ID, bias=K(NT5, 128))])
+    wait("t", V3E)
+    my0 = group("t", [mm(T.pe, 0, "aq", 0, "v3", 0, 322)])
+    wait("t", V3L)
+    my1 = group("t", [mm(T.pe, 1, "aq", 0, "v3", 322, 450)])
+    wait("s", my0)
+    Y0 = group("s", [act(T.ysb[:, 0:322], T.pe[:, 0:322], ACT.Copy)])
+    wait("s", my1)
+    Y1 = group("s", [act(T.ysb[:, 322:450], T.pe[:, 512:640], ACT.Copy)])
+
+    B2e, rest = border(2, CS2, MK2, M2, N2, False)
+    wait("v", B2e, ST, C5, C4e, C3)
+    th = [K(TH5, 128), K(TH4, 128), K(TH3, 128), K(TH2, 128), 32.0]
+    e = group("v", [ts(T.d0[:, 1 + s:196:7], T.jj[:], CN(4), A.add, th[s], A.is_ge) for s in range(5)] +
+              [ts(T.d0[:, 6:196:7], T.jm[:], CN(4), A.add, CN(5), A.is_lt), ts(T.d1[:, 5:196:7], T.jj[:], CN(4), A.add, 418.0, A.add)])
+    wait("v", e)
+    e = group("v", [lambda: V.tensor_tensor_scan(T.sc[:], T.d0[:], T.d1[:], 0.0, A.mult, A.add)])
+    wait("v", e)
+    O3 = group("v", [cp(T.of3[:], T.sc[:, 6:196:7])])
+    H = E // 2
+    half = [(H * h, H * h + H, T.of3[:, 14 * h:14 * h + 14]) for h in range(2)]
+    wait("v", O3, V3E, V3L)
+    wait("s", O3, Y0, Y1)
+    FC, FY = [], []
+    for lo, hi, off in half:
+        FC.append(group("v", [cp(T.fin[:, lo:hi].bitcast(dt.uint32), T.v3[:].bitcast(dt.uint32).indirect(off))]))
+        FY.append(group("s", [act(T.yo[:, lo:hi], T.ysb[:].indirect(off), ACT.Copy)]))
+        if lo == 0:
+            e = group("v", rest)
+        else:
+            wait("v", e)
+            e = columns(2)
+    FS = [group("v", [cp(T.fins[:, 0:H], T.v3s[:].indirect(half[0][2]))]),
+          group("s", [act(T.fins[:, H:E], T.v3s[:].indirect(half[1][2]), ACT.Copy)])]
+    wait("v", e)
+    e = group("v", [tr(T.bt[0:32, :], T.bh[0:32, :])])
+    wait("v", e)
+    e = group("v", [cp(T.bo[0:32, 0:N], T.bt[0:32, 0:32:4])])
+    for h, (lo, hi, off) in enumerate(half):
+        wait("y", FC[h])
+        dma("y", [(T.oc[:, 4 * lo:4 * hi], T.fin[:, lo:hi].bitcast(dt.uint8))])
+        wait("y", FY[h])
+        dma("y", [(T.y[:, lo:hi], T.yo[:, lo:hi])])
+    wait("s", *FS)
+    dma("s", [(T.osc[4 * k:4 * k + 4, :], T.fins[32 * k:32 * k + 4, :]) for k in range(2)])
+    wait("y", *FS)
+    dma("y", [(T.osc[4 * k:4 * k + 4, :], T.fins[32 * k:32 * k + 4, :]) for k in range(2, 4)])
+    wait("s", e)
+    dma("s", [(T.bd[:], T.bo[0:R, 0:N + 1])])
+
+    g.wait_ge(T.sem.sent, sent[0])
+    for name in total:
+        if max(seen[q].get(name, 0) for q in Q) < total[name]:
+            wait("g", (name, total[name]))

@@ -12,8 +12,8 @@ def _pair(name, n):
 
 SCRATCH = {
     "hx": ("sbuf", [128, 1024], BF), "ha": ("sbuf", [128, 512], BF), "hw": ("sbuf", [128, 2048], BF),
-    "h1": ("sbuf", [128, 1536], BF), "h2": ("sbuf", [128, 1536], BF), "h3": ("sbuf", [128, 1800], BF),
-    **_pair("xq", 320), **_pair("aq", 128), **_pair("wq", 512), **_pair("v1", 384), **_pair("v2", 384), **_pair("v3", 450),
+    "h1": ("sbuf", [128, 1536], BF), "h2": ("sbuf", [128, 1536], BF), "h3": ("sbuf", [128, 2056], BF),
+    **_pair("xe", 128), **_pair("xq", 320), **_pair("aq", 128), **_pair("wq", 512), **_pair("v1", 384), **_pair("v2", 384), **_pair("v3", 514),
     **_pair("ld1", 192), **_pair("ld2", 320), **_pair("p1", 192), **_pair("p2", 192), **_pair("fin", E),
     "pe": ("psum", [128, 2048], F32), "pl": ("psum", [128, 2048], F32),
     "junk": ("sbuf", [128, 1280], BF),
@@ -32,7 +32,7 @@ SCRATCH = {
     "of1": ("sbuf", [128, 4], U16), "of2": ("sbuf", [128, 4], U16), "of3": ("sbuf", [128, 28], U16),
     "t2": ("sbuf", [128, 8], F32), "d0": ("sbuf", [128, 196], F32), "d1": ("sbuf", [128, 196], F32), "sc": ("sbuf", [128, 196], F32),
 }
-POOL = {"v": 56, "s": 40, "t": 22, "g": 4, "d": 16}
+POOL = {"v": 54, "s": 40, "t": 22, "g": 4, "d": 20}
 SEMAPHORES = [q + str(i) for q in POOL for i in range(POOL[q])] + ["ex", "e1", "e2", "ga0", "ga1", "ga2", "sent"]
 
 A = AluOpType
@@ -168,7 +168,7 @@ def rank_program(g, core, T, topo):
         return T.k[0:p, i:i + 1]
     RHO, INN, BB, PM, CC, SIG, R127, LIM1, LIMP, LIMA, I0, AB, CS, COL0, SIGM, KK, K1, K2, K0, I130 = range(20)
     COLM, NB = 20, 24
-    TH2, TH3, TH4, TH5, KU, VV_, CL64, KR, K224, RR, NT5, EE = range(30, 42)
+    TH2, TH3, TH4, TH5, VV_, CL64, KR, K224, RR, NT5, EE, K64 = range(30, 42)
 
     def W(i):
         return T.cw[0:32, 128 * i:128 * i + 128]
@@ -180,9 +180,9 @@ def rank_program(g, core, T, topo):
     def CN(i, p=128):
         return T.cn[0:p, i:i + 1]
 
-    LX = dma("y", [(T.hx[:], T.x[:])])
+    LX = [dma("y", [(T.hx[:, 0:512], T.x[:, 512:1024])]), dma("s", [(T.hx[:, 512:1024], T.x[:, 0:512])])]
     LA = dma("y", [(T.ha[:], T.a[:])])
-    LW = [dma("y", [(T.hw[:, 512 * b:512 * b + 512], T.w[:, 512 * b:512 * b + 512])]) for b in range(4)]
+    LW = [dma("sy"[b % 2], [(T.hw[:, 512 * b:512 * b + 512], T.w[:, 512 * b:512 * b + 512])]) for b in range(4)]
 
     io = lambda o, p, b, c: (lambda: g.iota(o, p, b, c, allow_small_or_imprecise_dtypes=True))
     G1e = group("g", [lambda: g.iota(T.ci[:], [[1, 4]], 0, 1)])
@@ -217,7 +217,6 @@ def rank_program(g, core, T, topo):
                      act(K(I0), K(INN), ID, bias=-FAR, scale=FAR), act(K(I130), K(INN), ID, scale=130.0)])
     wait("s", L3, G3e, S1)
     S2 = group("s", [act(W(TP_), T.it[0:32, :], ID, bias=K(R127), scale=K(SIG)),
-                     act(M(0, 0), T.it[0:32, :], ID, bias=K(INN), scale=0.0),
                      act(M(0, 1), T.it[0:32, :], ID, bias=K(I130), scale=0.0),
                      act(T.sel[0:32, 0:64], T.sel[0:32, 96:160], ID, scale=0.5)])
 
@@ -227,11 +226,12 @@ def rank_program(g, core, T, topo):
         wait("s", e)
         return group("s", [act(M(t, 3), M(t, 2), ACT.Relu, bias=-16.0 * BIG, scale=BIG)])
 
-    wait("v", LX)
+    wait("v", *LX)
+    XE = group("v", [qz("xe", 0, 128, T.hx, 64)])
     XQ = group("v", [qz("xq", 0, 256, T.hx)])
-    wait("g", XQ)
+    wait("g", XE)
     lslot = lambda c: 256 if T.rank_of(c) == N - 1 else 288
-    edges("xq", "xq", ([(left, 0, 256, 32)] if left is not None else []) + ([(right, 224, lslot(right), 32)] if right is not None else []), "ex", True)
+    edges("xe", "xq", ([(left, 64, 256, 32)] if left is not None else []) + ([(right, 32, lslot(right), 32)] if right is not None else []), "ex", True)
     wait("v", LA)
     AQ = group("v", [qz("aq", 0, 128, T.ha)])
     wait("t", XQ, AQ)
@@ -240,7 +240,7 @@ def rank_program(g, core, T, topo):
     wait("s", FILL)
     for j in range(2):
         wait("s", mc[j])
-        CS0.append(group("s", [count(T.pl, j, T.land0, 1 + j)]))
+        CS0.append(group("s", [count(T.pl, j, T.land0, 2 - j)]))
     wait("g", FILL, *CS0)
     share(T.land0, "ga0")
 
@@ -261,7 +261,7 @@ def rank_program(g, core, T, topo):
             ts(W(INV2), W(ABT), K(LIMA), A.is_ge, -FAR, A.mult)],
            [tt(W(G1), W(G1R), W(INV1), A.add), qz("p1", 64, 192, T.hx, 0)],
            [tt(W(G2A), W(G2S), W(INV2), A.add), qz("p2", 64, 192, T.hx, 0)],
-           [tt(W(TPP), W(TM), W(INVP), A.add)]]
+           [tt(W(TPP), W(TM), W(INVP), A.add), ms(T.h3[:, 1800:2056], 0.0)]]
     WQ, GP = [], []
     for b in range(4):
         wait("v", LW[b])
@@ -271,19 +271,21 @@ def rank_program(g, core, T, topo):
             GP.append(group("v", gap[b - 1]))
 
     def early(ps, mq, lo, hi, tile, cuts, evs):
-        out = []
+        ms_ = []
         for b in range(4):
             wait("t", evs[b])
-            m = group("t", [mm(ps, b, "wq", 128 * b, mq, lo, hi)])
-            wait("s", m)
-            out.append(group("s", [evac("s", tile, b, at, ps, a, n) for a, at, n in cuts]))
-        return out
+            ms_.append(group("t", [mm(ps, b, "wq", 128 * b, mq, lo, hi)]))
 
-    def late(ps, mq, lo, tile, a, at, n):
+        def move(b):
+            wait("s", ms_[b])
+            return group("s", [evac("s", tile, b, at, ps, a, n) for a, at, n in cuts])
+        return move
+
+    def late(ps, mq, lo, tile, a, at, n, qs="sv"):
         ms_ = [group("t", [mm(ps, b, "wq", 128 * b, mq, lo, lo + 128)]) for b in range(4)]
         out = []
         for b in range(4):
-            q = "sv"[b % 2]
+            q = qs[b % 2]
             wait(q, ms_[b])
             out.append(group(q, [evac(q, tile, b, at, ps, a, n)]))
         return out
@@ -296,7 +298,8 @@ def rank_program(g, core, T, topo):
             out.append(group("s", [count(ps, bk, land, j)]))
         return out
 
-    ev = early(T.pe, "xq", 0, 256, T.h1, [(0, 224, 128), (128, 32, 128)], WQ)
+    mv = early(T.pe, "xq", 0, 256, T.h1, [(0, 32, 128), (128, 224, 128)], WQ)
+    ev = [mv(b) for b in range(4)]
     wait("v", *ev)
     V1E = group("v", [qz("v1", 0, 128, T.h1), qz("v1", 256, 384, T.h1)])
     GP.append(group("v", gap[3]))
@@ -316,13 +319,16 @@ def rank_program(g, core, T, topo):
     wait("g", *CS1)
     share(T.land1, "ga1")
 
-    def border(t, own, mask, mask130, bar, all_now, hole=None, after=None):
+    def border(t, own, mask, mask130, bar, hole, after):
         lt, sm, vv, cm = (b[0:32, 128 * t:128 * t + 128] for b in (T.lt, T.sm, T.vv, T.cmp))
         u0, x0, y0 = 132 * t, 64 * t, 96 * t
         wait("v", GA[t], *own)
         e = group("v", [tr(T.lt[0:32, 128 * t + 32 * a:128 * t + 32 * a + 32], lands[t][32 * a:32 * a + 32, :]) for a in range(4)])
-        wait("v", e, mask)
-        e = group("v", [tt(sm, lt, M(t, 0), A.mult)])
+        if mask is None:
+            sm = lt
+        else:
+            wait("v", e, mask)
+            e = group("v", [tt(sm, lt, M(t, 0), A.mult)])
         wait("v", e, mask130)
         e = group("v", [lambda: V.tensor_tensor_scan(T.uu[0:32, u0 + 1:u0 + 129], sm, M(t, 1), 0.0, A.add, A.add)])
         wait("v", e)
@@ -333,14 +339,12 @@ def rank_program(g, core, T, topo):
         ev_ = group("v", [tt(vv, T.uu[0:32, u0:u0 + 128], M(t, 3), A.add)])
         wait("v", e)
         e = group("v", [red(CN(8 + t, 32), T.xx[0:32, x0 + 32:x0 + 64])])
-        if hole:
-            hole()
+        hole()
         wait("s", e, ev_)
         e = group("s", [lambda: SC.activation(cm, vv, ACT.Sign, bias=CN(8 + t, 32), scale=-16.0, accum_out=CN(12 + t, 32))])
         wait("s", e)
         e = group("s", [act(T.yy[0:32, y0:y0 + 96], T.sel[0:32, 0:96], ID, bias=8.0, scale=CN(12 + t, 32))])
-        if after:
-            after()
+        after()
         wait("v", e)
         lo, hi = (32 if left is None else 0), (32 if right is None else 64)
         e = group("v", [tr(T.yt[0:32, y0 + lo:y0 + 96], T.yy[0:32, y0 + lo:y0 + 96])] +
@@ -348,7 +352,7 @@ def rank_program(g, core, T, topo):
         wait("v", e)
         own_ = [red(CN(2 * t + s), T.yt[:, y0 + 32 * s:y0 + 32 * s + 32]) for s in range(2) if (left, right)[s] is not None]
         rest = [red(CN(16 + t, 32), T.yt[0:32, y0 + 64:y0 + 96])]
-        return group("v", own_ + rest) if all_now else (group("v", own_), rest)
+        return group("v", own_), rest
 
     def columns(t):
         return group("v", [ts(T.bh[0:32, t:t + 1], CN(16 + t, 32), K(SIGM), A.mult, K(COLM + t), A.add)])
@@ -362,14 +366,10 @@ def rank_program(g, core, T, topo):
         e = group("s", [act(K(NB + t), T.bh[0:32, t - 1:t], ID, bias=-15.5, scale=-1.0), act(M(t, 1), M(t, 0), ID, scale=130.0)])
         return e, barrier(t, gs, e, *evs)
 
-    def pick(dst, src, n, off):
-        c = group("v", [cp(T[dst][:, 0:64].bitcast(dt.uint32), T[src][:, 0:n].bitcast(dt.uint32).indirect(off[:, 0:4]))])
-        s = group("s", [act(T[dst + "s"][:, 0:64], T[src + "s"][:, 0:n].indirect(off[:, 0:4]), ACT.Copy)])
-        return c, s
-
     box = {}
 
-    ev = early(T.pl, "v1", 32, 352, T.h2, [(0, 0, 160), (160, 224, 160)], [None] * 4)
+    mv = early(T.pl, "v1", 32, 352, T.h2, [(0, 0, 160), (160, 224, 160)], [None] * 4)
+    ev = [mv(b) for b in range(4)]
     wait("v", *GP)
 
     def hole1():
@@ -379,104 +379,113 @@ def rank_program(g, core, T, topo):
     def after1():
         wait("t", box["V2E"])
         box["CS2"] = costs(T.pl, (0, 1), "v2", T.land2, [(1, 256), (2, 0)])
-    B0 = border(0, CS0, S2, None, N0, True, hole1, after1)
+    B0, rest = border(0, CS0, None, S2, N0, hole1, after1)
     V2E, CS2 = box["V2E"], box["CS2"]
     wait("v", B0)
     j2 = T.jj[:, 0:2]
     O1 = group("v", [ts(T.of1[:, 0:2], j2, CN(1), A.add) if right is not None else ts(T.of1[:, 0:2], j2, 96.0, A.add),
                      ts(T.of1[:, 2:4], j2, CN(0), A.add, 96.0, A.add) if left is not None else ts(T.of1[:, 2:4], j2, 0.0, A.add)])
-    COL_0 = columns(0)
+    e = group("v", rest)
     wait("v", E1, O1)
     wait("s", E1, O1)
-    pk = pick("p1", "ld1", 192, T.of1)
+    pk = [group("v", [cp(T.p1[:, 0:64].bitcast(dt.uint32), T.ld1[:].bitcast(dt.uint32).indirect(T.of1[:, 0:4]))]),
+          group("s", [act(T.p1s[:, 0:64], T.ld1s[:].indirect(T.of1[:, 0:4]), ACT.Copy)])]
+    wait("v", e)
+    COL_0 = columns(0)
     MK1 = masks(1, W(G1), COL_0)
     wait("t", GP[1], *pk)
     wait("t", *CS1)
     ev = late(T.pe, "p1", 0, T.h2, 0, 160, 64)
     wait("v", *ev)
     V2L = group("v", [qz("v2", 128, 256, T.h2)])
-    wait("g", V2E, V2L)
-    edges("v2", "ld2", ([(left, 192, 0, 160)] if left is not None else []) + ([(right, 32, 160, 160)] if right is not None else []), "e2", False)
     wait("t", V2L)
     CS2 += costs(T.pl, (2, 3), "v2", T.land2, [(0, 192), (3, 64)])
     wait("g", *CS2)
     share(T.land2, "ga2")
+    wait("g", V2E, V2L)
+    edges("v2", "ld2", ([(left, 192, 0, 160)] if left is not None else []) + ([(right, 32, 160, 160)] if right is not None else []), "e2", False)
 
     M1, N1 = masks2(1, W(G1), COL_0, MK1, GP[1])
     c0 = T.bh[0:32, 0:1]
-    wait("s", GP[3])
-    BQe = group("s", [act(W(BQ), W(TPP), ID, bias=c0)])
-    ev = early(T.pe, "v2", 0, 384, T.h3, [(0, 2, 384)], [None] * 4)
-    e = group("v", [ts(W(B2), W(G2A), c0, A.is_lt, -FAR, A.mult)])
-    wait("v", e)
-    A2e = group("v", [tt(W(A2), W(G2A), W(B2), A.add)])
+    mv = early(T.pe, "v2", 0, 384, T.h3, [(0, 2, 384)], [None] * 4)
+    ev3 = [mv(0)]
 
     def hole2():
-        wait("v", A2e, BQe)
-        box["G2"] = group("v", [tt(W(G2), W(A2), W(BQ), A.max)])
-        wait("v", *ev)
-        box["V3E"] = group("v", [qz("v3", 0, 322, T.h3)])
+        e = group("v", [ts(W(B2), W(G2A), c0, A.is_lt, -FAR, A.mult)])
+        wait("v", e)
+        box["A2"] = group("v", [tt(W(A2), W(G2A), W(B2), A.add)])
 
     def after2():
-        wait("s", B0, L5)
+        wait("s", B0, L5, GP[3])
         box["C1"] = group("s", [act(K(COLM + 1), K(SIGM), ID, bias=c0, scale=-32.0), act(K(CL64, 128), CN(0), ID, bias=-64.0),
-                                act(K(KR, 128), CN(1), ID, bias=288.0), act(K(K224, 128), CN(0), ID, bias=224.0, scale=-1.0),
-                                act(T.d1[:, 1:196:7], T.neg[:], ID, bias=64.0, scale=CN(1)), act(T.d1[:, 3:196:7], T.neg[:], ID, bias=CN(0), scale=0.0)])
-        wait("s", box["C1"])
-        box["C2"] = group("s", [act(K(KU, 128), CN(0), ID, bias=K(KR, 128), scale=-1.0)])
-    B1 = border(1, CS1, MK1, M1, N1, True, hole2, after2)
-    V3E = box["V3E"]
-    wait("v", B1, box["C1"])
-    e = group("v", [ts(T.t2[:, 0:2], j2, CN(3), A.add, 32.0, A.is_ge), ts(T.t2[:, 2:4], j2, CN(2), A.add, 64.0, A.is_lt)])
+                                act(W(BQ), W(TPP), ID, bias=c0)])
+        ev3.append(mv(1))
+        ev3.append(mv(2))
+    B1, rest = border(1, CS1, MK1, M1, N1, hole2, after2)
+    e0 = group("v", rest)
+    wait("v", box["C1"], box["A2"])
+    G2e_ = group("v", [tt(W(G2), W(A2), W(BQ), A.max)])
+    wait("v", e0, B1)
     COL_1 = columns(1)
-    wait("s", B1, box["C2"])
-    C3 = group("s", [act(K(TH2, 128), CN(2), ID, bias=64.0, scale=-1.0), act(K(TH3, 128), CN(2), ID, bias=K(K224, 128), scale=-1.0),
-                     act(K(VV_, 128), CN(2), ID, bias=K(KU, 128), scale=-1.0), act(K(RR, 128), CN(3), ACT.Relu, bias=-32.0),
-                     act(T.d1[:, 0:196:7], T.neg[:], ID, bias=256.0, scale=CN(3))])
-    wait("s", C3)
-    C4e = group("s", [act(K(TH5, 128), CN(3), ID, bias=K(VV_, 128)), act(T.d1[:, 4:196:7], T.neg[:], ID, bias=-192.0, scale=K(TH2, 128))])
-    wait("v", e)
-    e = group("v", [ts(T.t2[:, 4:6], T.t2[:, 0:2], CN(1), A.mult, CN(3), A.add), ts(T.t2[:, 6:8], T.t2[:, 2:4], K(CL64, 128), A.mult, CN(2), A.add)])
-    wait("v", e)
+    e1 = group("v", [ts(K(K64, 128), CN(3), 64.0, A.add)] +
+               ([ts(T.t2[:, 0:2], j2, CN(3), A.add, 32.0, A.is_ge), ts(T.t2[:, 4:6], j2, CN(3), A.add)] if right is not None else []))
+    MK2 = masks(2, W(G2), COL_1, G2e_)
+    e = group("v", ([ts(T.t2[:, 2:4], j2, CN(2), A.add, 64.0, A.is_lt), ts(T.t2[:, 6:8], j2, CN(2), A.add, 224.0, A.add)] if left is not None else
+                    [ts(T.of2[:, 2:4], j2, 0.0, A.add)]))
+    wait("v", e, e1)
     o2 = []
     if right is not None:
-        o2 += [ts(T.of2[:, k:k + 1], T.t2[:, 4 + k:5 + k], K(PM, 128), A.add, 16.0 * k, A.add) for k in range(2)]
+        o2 += [ts(T.of2[:, k:k + 1], T.t2[:, k:k + 1], CN(1), A.mult, T.t2[:, 4 + k:5 + k], A.add) for k in range(2)]
     else:
         o2 += [ts(T.of2[:, 0:2], j2, 160.0, A.add)]
     if left is not None:
-        o2 += [ts(T.of2[:, 2 + k:3 + k], T.t2[:, 6 + k:7 + k], K(PM, 128), A.add, 224.0 + 16.0 * k, A.add) for k in range(2)]
-    else:
-        o2 += [ts(T.of2[:, 2:4], j2, 0.0, A.add)]
+        o2 += [ts(T.of2[:, 2 + k:3 + k], T.t2[:, 2 + k:3 + k], K(CL64, 128), A.mult, T.t2[:, 6 + k:7 + k], A.add) for k in range(2)]
     O2 = group("v", o2)
-    MK2 = masks(2, W(G2), COL_1, box["G2"])
-    wait("v", E2, O2)
-    wait("s", E2, O2)
-    pk = pick("p2", "ld2", 320, T.of2)
-    wait("t", GP[2], *pk)
-    wait("t", *CS2)
-    ev = late(T.pl, "p2", 0, T.h3, 0, 386, 64)
+    ev3.append(mv(3))
     M2, N2 = masks2(2, W(G2), COL_1, MK2)
-    wait("v", *ev)
-    V3L = group("v", [qz("v3", 322, 450, T.h3)])
-    wait("s", C4e)
-    C5 = group("s", [act(K(TH4, 128), K(RR, 128), ID, bias=K(TH5, 128), scale=-1.0), act(K(NT5, 128), K(TH5, 128), ID, bias=32.0, scale=-1.0),
+    wait("s", B1, e1)
+    C2 = group("s", [act(K(KR, 128), CN(1), ID, bias=K(K64, 128)), act(K(K224, 128), CN(0), ID, bias=224.0, scale=-1.0),
+                     act(K(TH2, 128), CN(2), ID, bias=64.0, scale=-1.0), act(K(RR, 128), CN(3), ACT.Relu, bias=-32.0)])
+    wait("s", C2)
+    e = group("s", [act(K(VV_, 128), K(K224, 128), ID, bias=K(KR, 128)), act(K(TH3, 128), CN(2), ID, bias=K(K224, 128), scale=-1.0),
+                    act(T.d1[:, 0:196:7], T.neg[:], ID, bias=256.0, scale=CN(3)), act(T.d1[:, 1:196:7], T.neg[:], ID, bias=64.0, scale=CN(1))])
+    wait("s", e)
+    e = group("s", [act(K(TH5, 128), CN(2), ID, bias=K(VV_, 128), scale=-1.0), act(T.d1[:, 3:196:7], T.neg[:], ID, bias=CN(0), scale=0.0),
+                    act(T.d1[:, 4:196:7], T.neg[:], ID, bias=-192.0, scale=K(TH2, 128))])
+    wait("s", e)
+    TH = group("s", [act(K(TH4, 128), K(RR, 128), ID, bias=K(TH5, 128), scale=-1.0), act(K(NT5, 128), K(TH5, 128), ID, bias=-32.0),
                      act(K(COLM + 2), K(SIGM), ID, bias=T.bh[0:32, 1:2], scale=-32.0)])
-    wait("s", C5)
-    ST = group("s", [act(T.jm[:], T.jj[:], ID, bias=K(NT5, 128))])
-    wait("t", V3E)
-    my0 = group("t", [mm(T.pe, 0, "aq", 0, "v3", 0, 322)])
-    wait("t", V3L)
-    my1 = group("t", [mm(T.pe, 1, "aq", 0, "v3", 322, 450)])
-    wait("s", my0)
-    Y0 = group("s", [act(T.ysb[:, 0:322], T.pe[:, 0:322], ACT.Copy)])
-    wait("s", my1)
-    Y1 = group("s", [act(T.ysb[:, 322:450], T.pe[:, 512:640], ACT.Copy)])
+    wait("s", TH, L3)
+    JM = group("s", [act(T.jm[:], T.jj[:], ID, bias=K(NT5, 128), scale=-1.0)])
 
-    B2e, rest = border(2, CS2, MK2, M2, N2, False)
-    wait("v", B2e, ST, C5, C4e, C3)
+    def hole3():
+        wait("v", *ev3)
+        box["V3E"] = group("v", [qz("v3", 0, 386, T.h3)])
+        wait("v", E2, O2)
+        box["PC"] = group("v", [cp(T.p2[:, 0:64].bitcast(dt.uint32), T.ld2[:].bitcast(dt.uint32).indirect(T.of2[:, 0:4]))])
+
+    def after3():
+        wait("s", E2, O2)
+        ps = group("s", [act(T.p2s[:, 0:64], T.ld2s[:].indirect(T.of2[:, 0:4]), ACT.Copy)])
+        wait("t", GP[2], box["PC"], ps, *CS2)
+        box["L3"] = late(T.pl, "p2", 0, T.h3, 0, 386, 64, "ss")
+        wait("t", box["V3E"])
+        my0 = group("t", [mm(T.pe, 0, "aq", 0, "v3", 0, 386)])
+        wait("s", my0)
+        box["Y0"] = group("s", [act(T.ysb[:, 0:386], T.pe[:, 0:386], ACT.Copy)])
+
+    B2e, rest = border(2, CS2, MK2, M2, N2, hole3, after3)
+    V3E, Y0 = box["V3E"], box["Y0"]
+    wait("v", B2e, JM)
     th = [K(TH5, 128), K(TH4, 128), K(TH3, 128), K(TH2, 128), 32.0]
     e = group("v", [ts(T.d0[:, 1 + s:196:7], T.jj[:], CN(4), A.add, th[s], A.is_ge) for s in range(5)] +
-              [ts(T.d0[:, 6:196:7], T.jm[:], CN(4), A.add, CN(5), A.is_lt), ts(T.d1[:, 5:196:7], T.jj[:], CN(4), A.add, 418.0, A.add)])
+              [ts(T.d0[:, 6:196:7], T.jm[:], CN(5), A.add, CN(4), A.is_gt), ts(T.d1[:, 5:196:7], T.jj[:], CN(4), A.add, 418.0, A.add)])
+    wait("v", *box["L3"])
+    V3L = group("v", [qz("v3", 386, 514, T.h3)])
+    wait("t", V3L)
+    my1 = group("t", [mm(T.pe, 1, "aq", 0, "v3", 386, 514)])
+    wait("s", my1)
+    Y1 = group("s", [act(T.ysb[:, 386:450], T.pe[:, 512:576], ACT.Copy)])
     wait("v", e)
     e = group("v", [lambda: V.tensor_tensor_scan(T.sc[:], T.d0[:], T.d1[:], 0.0, A.mult, A.add)])
     wait("v", e)
@@ -484,18 +493,18 @@ def rank_program(g, core, T, topo):
     H = E // 2
     half = [(H * h, H * h + H, T.of3[:, 14 * h:14 * h + 14]) for h in range(2)]
     wait("v", O3, V3E, V3L)
-    wait("s", O3, Y0, Y1)
+    wait("s", O3, Y0, Y1, V3E, V3L)
     FC, FY = [], []
     for lo, hi, off in half:
-        FC.append(group("v", [cp(T.fin[:, lo:hi].bitcast(dt.uint32), T.v3[:].bitcast(dt.uint32).indirect(off))]))
+        FC.append(group("v", [cp(T.fin[:, lo:hi].bitcast(dt.uint32), T.v3[:, 0:450].bitcast(dt.uint32).indirect(off))]))
         FY.append(group("s", [act(T.yo[:, lo:hi], T.ysb[:].indirect(off), ACT.Copy)]))
         if lo == 0:
             e = group("v", rest)
         else:
             wait("v", e)
             e = columns(2)
-    FS = [group("v", [cp(T.fins[:, 0:H], T.v3s[:].indirect(half[0][2]))]),
-          group("s", [act(T.fins[:, H:E], T.v3s[:].indirect(half[1][2]), ACT.Copy)])]
+    FS = [group("v", [cp(T.fins[:, 0:H], T.v3s[:, 0:450].indirect(half[0][2]))]),
+          group("s", [act(T.fins[:, H:E], T.v3s[:, 0:450].indirect(half[1][2]), ACT.Copy)])]
     wait("v", e)
     e = group("v", [tr(T.bt[0:32, :], T.bh[0:32, :])])
     wait("v", e)
@@ -503,8 +512,11 @@ def rank_program(g, core, T, topo):
     for h, (lo, hi, off) in enumerate(half):
         wait("y", FC[h])
         dma("y", [(T.oc[:, 4 * lo:4 * hi], T.fin[:, lo:hi].bitcast(dt.uint8))])
-        wait("y", FY[h])
-        dma("y", [(T.y[:, lo:hi], T.yo[:, lo:hi])])
+        if h == 0:
+            wait("y", FY[h])
+            dma("y", [(T.y[:, lo:hi], T.yo[:, lo:hi])])
+    wait("s", FY[1])
+    dma("s", [(T.y[:, H:E], T.yo[:, H:E])])
     wait("s", *FS)
     dma("s", [(T.osc[4 * k:4 * k + 4, :], T.fins[32 * k:32 * k + 4, :]) for k in range(2)])
     wait("y", *FS)

from concourse.bass import DstId, RemoteDMATransfer
from concourse.mybir import dt, AluOpType, AxisListType, ActivationFunctionType

N, P, S, R = 8, 256, 32, 3
E = P + 2 * S * R
C4, U8, F32, BF, I32, U16 = "float8_e4m3fn_x4", "uint8", "float32", "bfloat16", "int32", "uint16"


def _pair(name, n):
    return {name: ("sbuf", [128, n], C4), name + "s": ("sbuf", [128, n], U8)}


SCRATCH = {
    "hx": ("sbuf", [128, 1024], BF), "ha": ("sbuf", [128, 512], BF), "hw": ("sbuf", [128, 2048], BF),
    "h1": ("sbuf", [128, 1536], BF), "h2": ("sbuf", [128, 1536], BF), "h3": ("sbuf", [128, 2056], BF),
    **_pair("xe", 128), **_pair("xq", 320), **_pair("aq", 128), **_pair("wq", 512), **_pair("v1", 384), **_pair("v2", 384), **_pair("v3", 514),
    **_pair("ld1", 192), **_pair("ld2", 320), **_pair("p1", 192), **_pair("p2", 192), **_pair("fin", E),
    "pe": ("psum", [128, 2048], F32), "pl": ("psum", [128, 2048], F32),
    "junk": ("sbuf", [128, 1280], BF),
    "land0": ("sbuf", [128, 32], F32), "land1": ("sbuf", [128, 32], F32), "land2": ("sbuf", [128, 32], F32),
    "ysb": ("sbuf", [128, 450], F32), "yo": ("sbuf", [128, E], F32),
    "ci": ("sbuf", [128, 4], I32), "ri": ("sbuf", [128, 4], I32), "k": ("sbuf", [128, 64], F32),
    "it": ("sbuf", [128, 128], F32), "brow": ("sbuf", [128, 36], F32), "dd": ("sbuf", [128, 32], F32),
    "a16": ("sbuf", [128, 28], F32), "jj": ("sbuf", [128, 28], F32), "jm": ("sbuf", [128, 28], F32),
    "zero": ("sbuf", [128, 32], F32), "neg": ("sbuf", [128, 28], F32), "sel": ("sbuf", [128, 160], F32), "mx": ("sbuf", [128, 96], F32),
    "cw": ("sbuf", [128, 128 * 16], F32),
    "msk": ("sbuf", [128, 128 * 12], F32),
    "lt": ("sbuf", [128, 128 * 3], F32), "sm": ("sbuf", [128, 128 * 3], F32), "uu": ("sbuf", [128, 132 * 3], F32),
    "vv": ("sbuf", [128, 128 * 3], F32), "cmp": ("sbuf", [128, 128 * 3], F32),
    "xx": ("sbuf", [128, 64 * 3], F32), "yy": ("sbuf", [128, 96 * 3], F32), "yt": ("sbuf", [128, 96 * 3], F32),
    "cn": ("sbuf", [128, 32], F32), "bh": ("sbuf", [128, 32], F32), "bt": ("sbuf", [128, 32], F32), "bo": ("sbuf", [128, 16], F32),
    "of1": ("sbuf", [128, 4], U16), "of2": ("sbuf", [128, 4], U16), "of3": ("sbuf", [128, 28], U16),
    "t2": ("sbuf", [128, 8], F32), "d0": ("sbuf", [128, 196], F32), "d1": ("sbuf", [128, 196], F32), "sc": ("sbuf", [128, 196], F32),
}
POOL = {"v": 54, "s": 40, "t": 22, "g": 4, "d": 20}
SEMAPHORES = [q + str(i) for q in POOL for i in range(POOL[q])] + ["ex", "e1", "e2", "ga0", "ga1", "ga2", "sent"]

A = AluOpType
ACT = ActivationFunctionType
FAR = 65536.0
BIG = 2097152.0
TINY = 2.0 ** -120


def rank_program(g, core, T, topo):
    r = T.rank_of(core)
    if r is None:
        return
    cores = T.cores
    left = cores[r - 1] if r > 0 else None
    right = cores[r + 1] if r < N - 1 else None
    V, SC, PE, SY = g.vector, g.scalar, g.tensor, g.sync
    Q = {"v": V, "s": SC, "t": PE, "g": g, "y": SY}
    ID = ACT.Identity

    total, seen, nxt = {}, {q: {} for q in Q}, {q: 0 for q in POOL}

    def wait(q, *evs):
        for ev in evs:
            if ev is not None and seen[q].get(ev[0], 0) < ev[1]:
                Q[q].wait_ge(T.sem[ev[0]], ev[1])
                seen[q][ev[0]] = ev[1]

    def group(q, calls, pool=None, inc=1):
        pool = pool or q
        name = pool + str(nxt[pool] % POOL[pool])
        nxt[pool] += 1
        if total.get(name, 0):
            wait(q, (name, total[name]))
        for c in calls:
            c().then_inc(T.sem[name], inc)
            total[name] = total.get(name, 0) + inc
        return (name, total[name])

    def dma(q, pairs):
        return group(q, [(lambda o=o, i=i: Q[q].dma_start(o, i)) for o, i in pairs], pool="d", inc=16)

    def ts(out, in0, s1, op0, s2=None, op1=None):
        if op1 is None:
            return lambda: V.tensor_scalar(out, in0, s1, None, op0)
        return lambda: V.tensor_scalar(out, in0, s1, s2, op0, op1)

    def tt(out, a, b, op):
        return lambda: V.tensor_tensor(out, a, b, op)

    def cp(out, a):
        return lambda: V.tensor_copy(out, a)

    def ms(out, c):
        return lambda: V.memset(out, c)

    def red(out, a):
        return lambda: V.tensor_reduce(out, a, AxisListType.X, A.add)

    def tr(out, a):
        return lambda: V.transpose(out, a)

    def act(out, a, f, bias=0.0, scale=1.0):
        if f == ACT.Copy:
            return lambda: SC.activation(out, a, f)
        return lambda: SC.activation(out, a, f, bias=bias, scale=scale)

    def qz(q, lo, hi, tile, at=None):
        at = lo if at is None else at
        return lambda: V.quantize_mx(T[q][:, lo:hi], T[q + "s"][:, lo:hi], tile[:, 4 * at:4 * (at + hi - lo)])

    def mm(ps, bank, sq, s0, mq, lo, hi):
        return lambda: PE.matmul_mx(ps[:, 512 * bank:512 * bank + hi - lo], T[sq][:, s0:s0 + 128], T[sq + "s"][:, s0:s0 + 128],
                                    T[mq][:, lo:hi], T[mq + "s"][:, lo:hi], True, True)

    def evac(q, tile, b, at, ps, lo, n):
        o, i = tile[:, 4 * at + b:4 * (at + n):4], ps[:, 512 * b + lo:512 * b + lo + n]
        return act(o, i, ACT.Relu, scale=0.0625) if q == "s" else ts(o, i, 0.0, A.max, 0.0625, A.mult)

    nj = [0]

    def count(ps, bank, land, j):
        jk = T.junk[:, 128 * nj[0]:128 * nj[0] + 128]
        nj[0] += 1
        return lambda: SC.activation(jk, ps[:, 512 * bank:512 * bank + 128], ACT.Sign, bias=-TINY, scale=1.0,
                                     accum_out=land[:, 4 * r + j:4 * r + j + 1])

    others = [c for c in cores if c != core]
    far = [c for c in others if topo.chip(c) != topo.chip(core)]
    far.sort(key=lambda c: topo.same_plane(topo.chip(c), topo.chip(core)) or topo.mates(topo.chip(c), topo.chip(core)))
    near = [c for c in others if topo.chip(c) == topo.chip(core)]

    def engines(src, dst):
        if topo.chip(src) != topo.chip(dst):
            return topo.engines(src, dst)
        out = [c for c in cores if topo.chip(c) != topo.chip(src)][0]
        return [e for e in topo.engines(src, dst) if e not in topo.engines(src, out)]

    sent = [0]

    def xfer(dsts, src, dst, sem):
        en = engines(core, dsts[0])
        sent[0] += len(en)
        return RemoteDMATransfer(dst_ids=[DstId(rid=topo.addr(c)[0], pnc=topo.addr(c)[1]) for c in dsts],
                                 dma_engine_mask=sum(1 << e for e in en), remote_sem=T.sem[sem], srcs=[src], dsts=[dst for c in dsts])

    def fused(trs):
        g.remote_dma_fused(trs, local_sem=T.sem.sent)

    def edges(src, dst, moves, sem, split):
        moves = sorted(moves, key=lambda m: m[0] in near)
        for plane in (False, True):
            trs = []
            for c, a, b, n in moves:
                if plane:
                    trs.append(xfer([c], T[src + "s"][:, a:a + n], T[dst + "s"][:, b:b + n], sem))
                else:
                    trs.append(xfer([c], T[src][:, a:a + n].bitcast(dt.uint8), T[dst][:, b:b + n].bitcast(dt.uint8), sem))
            for part in ([[t] for t in trs] if split else [trs]):
                fused(part)

    def share(land, sem):
        v = land[:, 4 * r:4 * r + 4]
        fused([xfer(far, v, v, sem), xfer(near, v, v, sem)])

    n_edge = sum(2 * len(engines(c, core)) for c in (left, right) if c is not None)
    n_all = sum(len(engines(c, core)) for c in others)
    EX, E1, E2 = ("ex", n_edge), ("e1", n_edge), ("e2", n_edge)
    GA = [("ga%d" % t, n_all) for t in range(R)]
    lands = [T.land0, T.land1, T.land2]

    def K(i, p=32):
        return T.k[0:p, i:i + 1]
    RHO, INN, BB, PM, CC, SIG, R127, LIM1, LIMP, LIMA, I0, AB, CS, COL0, SIGM, KK, K1, K2, K0, I130 = range(20)
    COLM, NB = 20, 24
    TH2, TH3, TH4, TH5, VV_, CL64, KR, K224, RR, NT5, EE, K64 = range(30, 42)

    def W(i):
        return T.cw[0:32, 128 * i:128 * i + 128]
    TP_, G1R, G2S, G0, INV1, INVP, ABT, INV2, G1, G2A, TPP, B2, BQ, A2, G2, TM = range(16)

    def M(t, i):
        return T.msk[0:32, 128 * (4 * t + i):128 * (4 * t + i) + 128]

    def CN(i, p=128):
        return T.cn[0:p, i:i + 1]

    LX = [dma("y", [(T.hx[:, 0:512], T.x[:, 512:1024])]), dma("s", [(T.hx[:, 512:1024], T.x[:, 0:512])])]
    LA = dma("y", [(T.ha[:], T.a[:])])
    LW = [dma("sy"[b % 2], [(T.hw[:, 512 * b:512 * b + 512], T.w[:, 512 * b:512 * b + 512])]) for b in range(4)]

    io = lambda o, p, b, c: (lambda: g.iota(o, p, b, c, allow_small_or_imprecise_dtypes=True))
    G1e = group("g", [lambda: g.iota(T.ci[:], [[1, 4]], 0, 1)])
    G2e = group("g", [io(T.brow[0:32, :], [[1, 9], [0, 4]], 0, 0), io(T.dd[0:32, :], [[1, 32]], 0, -1), io(T.a16[:], [[16, 28]], 0, 0)])
    G3e = group("g", [io(T.it[0:32, :], [[1, 128]], 0, 0)])

    fills = [ms(T.zero[:], 0.0), ms(T.neg[:], -1.0), ms(T.land0[:, 4 * r:4 * r + 4], 0.0), ms(T.h1[:, 0:128], 0.0), ms(T.h1[:, 1408:1536], 0.0),
             ms(T.bh[0:32, :], 0.0), ms(T.bo[0:32, :], float(N * P)), ms(T.uu[0:32, 0:396:132], 0.0), ms(T.h3[:, 0:8], 0.0),
             ms(T.d0[:, 0:196:7], 0.0), ms(T.d1[:, 6:196:7], 0.0), ms(T.d1[:, 2:196:7], -384.0)]
    if left is None:
        fills += [ms(T.cn[:, 0:6:2], float(S)), ms(T.h1[:, 4 * 192:4 * 224], 0.0)]
    if right is None:
        fills += [ms(T.cn[:, 1:6:2], float(S)), ms(T.h1[:, 4 * 160:4 * 192], 0.0)]
    FILL = group("v", fills)
    wait("v", G1e)
    e = group("v", [ts(T.ri[:, 0:2], T.ci[:, 0:2], 1, A.arith_shift_right, 1, A.bitwise_and),
                    ts(T.ri[:, 2:3], T.ci[:, 2:3], 2, A.arith_shift_right), ts(T.ri[:, 3:4], T.ci[:, 0:1], 15, A.bitwise_and),
                    cp(K(CC, 128), T.ci[:, 0:1])])
    wait("v", e)
    KF = group("v", [cp(T.k[:, 0:4], T.ri[:])])
    wait("v", KF, G2e, FILL)
    brow = T.brow[0:32, 2:34]
    L3 = group("v", [ts(K(SIG), K(RHO), -2.0, A.mult, 1.0, A.add), ts(K(R127), K(RHO), 127.0, A.mult),
                     ts(T.jj[:], T.a16[:], K(PM, 128), A.add),
                     ts(T.sel[0:32, 96:128], T.zero[0:32, :], K(BB), A.add, float(r), A.is_equal),
                     ts(T.sel[0:32, 128:160], T.zero[0:32, :], K(BB), A.add, float(r + 1), A.is_equal),
                     ts(T.sel[0:32, 64:96], brow, K(BB), A.is_equal, 0.5, A.mult),
                     ts(T.mx[0:32, 32:64], T.dd[0:32, :], 0.0, A.is_gt, 16.0, A.mult), ts(T.mx[0:32, 64:96], brow, 16.0 / N, A.mult)])
    wait("s", KF, e)
    S1 = group("s", [act(K(AB), K(CC), ACT.Abs, bias=-15.5), act(K(LIM1), K(INN), ID, bias=64.0, scale=32.0),
                     act(K(LIMP), K(INN), ID, bias=32.0, scale=-32.0), act(K(LIMA), K(INN), ID, bias=16.0, scale=1000.0),
                     act(K(I0), K(INN), ID, bias=-FAR, scale=FAR), act(K(I130), K(INN), ID, scale=130.0)])
    wait("s", L3, G3e, S1)
    S2 = group("s", [act(W(TP_), T.it[0:32, :], ID, bias=K(R127), scale=K(SIG)),
                     act(M(0, 1), T.it[0:32, :], ID, bias=K(I130), scale=0.0),
                     act(T.sel[0:32, 0:64], T.sel[0:32, 96:160], ID, scale=0.5)])

    def barrier(t, gs, *evs):
        wait("s", *evs)
        e = group("s", [act(M(t, 2), gs, ACT.Abs, bias=K(NB + t))])
        wait("s", e)
        return group("s", [act(M(t, 3), M(t, 2), ACT.Relu, bias=-16.0 * BIG, scale=BIG)])

    wait("v", *LX)
    XE = group("v", [qz("xe", 0, 128, T.hx, 64)])
    XQ = group("v", [qz("xq", 0, 256, T.hx)])
    wait("g", XE)
    lslot = lambda c: 256 if T.rank_of(c) == N - 1 else 288
    edges("xe", "xq", ([(left, 64, 256, 32)] if left is not None else []) + ([(right, 32, lslot(right), 32)] if right is not None else []), "ex", True)
    wait("v", LA)
    AQ = group("v", [qz("aq", 0, 128, T.ha)])
    wait("t", XQ, AQ)
    mc = [group("t", [mm(T.pl, j, "xq", 128 * j, "aq", 0, 128)]) for j in range(2)]
    CS0 = []
    wait("s", FILL)
    for j in range(2):
        wait("s", mc[j])
        CS0.append(group("s", [count(T.pl, j, T.land0, 2 - j)]))
    wait("g", FILL, *CS0)
    share(T.land0, "ga0")

    wait("v", L3, S1)
    L4 = group("v", [ts(K(CS), K(CC), K(SIG), A.mult, 64.0, A.mult), ts(K(COL0), K(BB), K(SIG), A.mult, float(P), A.mult),
                     ts(K(SIGM), K(AB), 14.0, A.is_lt, K(SIG), A.mult), tt(T.mx[0:32, 0:32], T.mx[0:32, 64:96], T.mx[0:32, 32:64], A.subtract)])
    wait("v", L4)
    L5 = group("v", [ts(K(KK), K(RHO), -64.0, A.mult, K(CS), A.add), ts(K(COLM), K(SIGM), -32.0, A.mult, K(COL0), A.add),
                     ts(K(NB), K(COL0), -1.0, A.mult, -15.5, A.add), ts(K(EE), K(CC), 0.0, A.is_equal, -1.0, A.mult)])
    wait("v", L5)
    L6 = group("v", [ts(K(K1), K(KK), -32.0, A.add), ts(K(K2), K(KK), -64.0, A.add), ts(K(K0), K(KK), -64.0, A.add, K(I0), A.add)])
    wait("s", S2, L6)
    S3 = group("s", [act(W(ABT), W(TP_), ACT.Abs, bias=-47.5), act(W(G1R), W(TP_), ID, bias=K(K1)),
                     act(W(G2S), W(TP_), ID, bias=K(K2)), act(W(G0), W(TP_), ID, bias=K(K0)), act(W(TM), W(TP_), ID, bias=-32.0)])
    N0 = barrier(0, W(G0), S3, L5)

    gap = [[ts(W(INV1), W(TP_), K(LIM1), A.is_ge, -FAR, A.mult), ts(W(INVP), W(TP_), K(LIMP), A.is_ge, -2 * FAR, A.mult),
            ts(W(INV2), W(ABT), K(LIMA), A.is_ge, -FAR, A.mult)],
           [tt(W(G1), W(G1R), W(INV1), A.add), qz("p1", 64, 192, T.hx, 0)],
           [tt(W(G2A), W(G2S), W(INV2), A.add), qz("p2", 64, 192, T.hx, 0)],
           [tt(W(TPP), W(TM), W(INVP), A.add), ms(T.h3[:, 1800:2056], 0.0)]]
    WQ, GP = [], []
    for b in range(4):
        wait("v", LW[b])
        WQ.append(group("v", [qz("wq", 128 * b, 128 * b + 128, T.hw)]))
        if b:
            wait("v", S3, *GP[:1])
            GP.append(group("v", gap[b - 1]))

    def early(ps, mq, lo, hi, tile, cuts, evs):
        ms_ = []
        for b in range(4):
            wait("t", evs[b])
            ms_.append(group("t", [mm(ps, b, "wq", 128 * b, mq, lo, hi)]))

        def move(b):
            wait("s", ms_[b])
            return group("s", [evac("s", tile, b, at, ps, a, n) for a, at, n in cuts])
        return move

    def late(ps, mq, lo, tile, a, at, n, qs="sv"):
        ms_ = [group("t", [mm(ps, b, "wq", 128 * b, mq, lo, lo + 128)]) for b in range(4)]
        out = []
        for b in range(4):
            q = qs[b % 2]
            wait(q, ms_[b])
            out.append(group(q, [evac(q, tile, b, at, ps, a, n)]))
        return out

    def costs(ps, banks, vq, land, chunks):
        ms_ = [group("t", [mm(ps, bk, vq, c0, "aq", 0, 128)]) for bk, (j, c0) in zip(banks, chunks)]
        out = []
        for m, bk, (j, c0) in zip(ms_, banks, chunks):
            wait("s", m)
            out.append(group("s", [count(ps, bk, land, j)]))
        return out

    mv = early(T.pe, "xq", 0, 256, T.h1, [(0, 32, 128), (128, 224, 128)], WQ)
    ev = [mv(b) for b in range(4)]
    wait("v", *ev)
    V1E = group("v", [qz("v1", 0, 128, T.h1), qz("v1", 256, 384, T.h1)])
    GP.append(group("v", gap[3]))
    wait("t", EX, *CS0)
    if left is not None and right is not None:
        ev = late(T.pl, "xq", 192, T.h1, 64, 160, 64)
    else:
        ev = late(T.pl, "xq", 160, T.h1, 96, 160 if left is None else 192, 32)
    wait("v", *ev)
    V1L = group("v", [qz("v1", 128, 256, T.h1)])
    wait("g", V1E, V1L)
    edges("v1", "ld1", ([(left, 192, 0, 96)] if left is not None else []) + ([(right, 96, 96, 96)] if right is not None else []), "e1", False)
    wait("t", V1E)
    CS1 = costs(T.pe, (0, 1), "v1", T.land1, [(1, 256), (2, 0)])
    wait("t", V1L)
    CS1 += costs(T.pe, (2, 3), "v1", T.land1, [(0, 192), (3, 64)])
    wait("g", *CS1)
    share(T.land1, "ga1")

    def border(t, own, mask, mask130, bar, hole, after):
        lt, sm, vv, cm = (b[0:32, 128 * t:128 * t + 128] for b in (T.lt, T.sm, T.vv, T.cmp))
        u0, x0, y0 = 132 * t, 64 * t, 96 * t
        wait("v", GA[t], *own)
        e = group("v", [tr(T.lt[0:32, 128 * t + 32 * a:128 * t + 32 * a + 32], lands[t][32 * a:32 * a + 32, :]) for a in range(4)])
        if mask is None:
            sm = lt
        else:
            wait("v", e, mask)
            e = group("v", [tt(sm, lt, M(t, 0), A.mult)])
        wait("v", e, mask130)
        e = group("v", [lambda: V.tensor_tensor_scan(T.uu[0:32, u0 + 1:u0 + 129], sm, M(t, 1), 0.0, A.add, A.add)])
        wait("v", e)
        e = group("v", [ts(T.xx[0:32, x0:x0 + 32], T.mx[0:32, 0:32], T.uu[0:32, u0 + 128:u0 + 129], A.mult, K(EE), A.add)])
        wait("v", e)
        e = group("v", [tr(T.xx[0:32, x0 + 32:x0 + 64], T.xx[0:32, x0:x0 + 32])])
        wait("v", bar)
        ev_ = group("v", [tt(vv, T.uu[0:32, u0:u0 + 128], M(t, 3), A.add)])
        wait("v", e)
        e = group("v", [red(CN(8 + t, 32), T.xx[0:32, x0 + 32:x0 + 64])])
        hole()
        wait("s", e, ev_)
        e = group("s", [lambda: SC.activation(cm, vv, ACT.Sign, bias=CN(8 + t, 32), scale=-16.0, accum_out=CN(12 + t, 32))])
        wait("s", e)
        e = group("s", [act(T.yy[0:32, y0:y0 + 96], T.sel[0:32, 0:96], ID, bias=8.0, scale=CN(12 + t, 32))])
        after()
        wait("v", e)
        lo, hi = (32 if left is None else 0), (32 if right is None else 64)
        e = group("v", [tr(T.yt[0:32, y0 + lo:y0 + 96], T.yy[0:32, y0 + lo:y0 + 96])] +
                  [tr(T.yt[32 * a:32 * a + 32, y0 + lo:y0 + hi], T.yy[0:32, y0 + lo:y0 + hi]) for a in range(1, 4)])
        wait("v", e)
        own_ = [red(CN(2 * t + s), T.yt[:, y0 + 32 * s:y0 + 32 * s + 32]) for s in range(2) if (left, right)[s] is not None]
        rest = [red(CN(16 + t, 32), T.yt[0:32, y0 + 64:y0 + 96])]
        return group("v", own_), rest

    def columns(t):
        return group("v", [ts(T.bh[0:32, t:t + 1], CN(16 + t, 32), K(SIGM), A.mult, K(COLM + t), A.add)])

    def masks(t, gs, col, *evs):
        wait("v", col, *evs)
        return group("v", [ts(M(t, 0), gs, T.bh[0:32, t - 1:t], A.is_ge)])

    def masks2(t, gs, col, m, *evs):
        wait("s", col, m)
        e = group("s", [act(K(NB + t), T.bh[0:32, t - 1:t], ID, bias=-15.5, scale=-1.0), act(M(t, 1), M(t, 0), ID, scale=130.0)])
        return e, barrier(t, gs, e, *evs)

    box = {}

    mv = early(T.pl, "v1", 32, 352, T.h2, [(0, 0, 160), (160, 224, 160)], [None] * 4)
    ev = [mv(b) for b in range(4)]
    wait("v", *GP)

    def hole1():
        wait("v", *ev)
        box["V2E"] = group("v", [qz("v2", 0, 128, T.h2), qz("v2", 256, 384, T.h2)])

    def after1():
        wait("t", box["V2E"])
        box["CS2"] = costs(T.pl, (0, 1), "v2", T.land2, [(1, 256), (2, 0)])
    B0, rest = border(0, CS0, None, S2, N0, hole1, after1)
    V2E, CS2 = box["V2E"], box["CS2"]
    wait("v", B0)
    j2 = T.jj[:, 0:2]
    O1 = group("v", [ts(T.of1[:, 0:2], j2, CN(1), A.add) if right is not None else ts(T.of1[:, 0:2], j2, 96.0, A.add),
                     ts(T.of1[:, 2:4], j2, CN(0), A.add, 96.0, A.add) if left is not None else ts(T.of1[:, 2:4], j2, 0.0, A.add)])
    e = group("v", rest)
    wait("v", E1, O1)
    wait("s", E1, O1)
    pk = [group("v", [cp(T.p1[:, 0:64].bitcast(dt.uint32), T.ld1[:].bitcast(dt.uint32).indirect(T.of1[:, 0:4]))]),
          group("s", [act(T.p1s[:, 0:64], T.ld1s[:].indirect(T.of1[:, 0:4]), ACT.Copy)])]
    wait("v", e)
    COL_0 = columns(0)
    MK1 = masks(1, W(G1), COL_0)
    wait("t", GP[1], *pk)
    wait("t", *CS1)
    ev = late(T.pe, "p1", 0, T.h2, 0, 160, 64)
    wait("v", *ev)
    V2L = group("v", [qz("v2", 128, 256, T.h2)])
    wait("t", V2L)
    CS2 += costs(T.pl, (2, 3), "v2", T.land2, [(0, 192), (3, 64)])
    wait("g", *CS2)
    share(T.land2, "ga2")
    wait("g", V2E, V2L)
    edges("v2", "ld2", ([(left, 192, 0, 160)] if left is not None else []) + ([(right, 32, 160, 160)] if right is not None else []), "e2", False)

    M1, N1 = masks2(1, W(G1), COL_0, MK1, GP[1])
    c0 = T.bh[0:32, 0:1]
    mv = early(T.pe, "v2", 0, 384, T.h3, [(0, 2, 384)], [None] * 4)
    ev3 = [mv(0)]

    def hole2():
        e = group("v", [ts(W(B2), W(G2A), c0, A.is_lt, -FAR, A.mult)])
        wait("v", e)
        box["A2"] = group("v", [tt(W(A2), W(G2A), W(B2), A.add)])

    def after2():
        wait("s", B0, L5, GP[3])
        box["C1"] = group("s", [act(K(COLM + 1), K(SIGM), ID, bias=c0, scale=-32.0), act(K(CL64, 128), CN(0), ID, bias=-64.0),
                                act(W(BQ), W(TPP), ID, bias=c0)])
        ev3.append(mv(1))
        ev3.append(mv(2))
    B1, rest = border(1, CS1, MK1, M1, N1, hole2, after2)
    e0 = group("v", rest)
    wait("v", box["C1"], box["A2"])
    G2e_ = group("v", [tt(W(G2), W(A2), W(BQ), A.max)])
    wait("v", e0, B1)
    COL_1 = columns(1)
    e1 = group("v", [ts(K(K64, 128), CN(3), 64.0, A.add)] +
               ([ts(T.t2[:, 0:2], j2, CN(3), A.add, 32.0, A.is_ge), ts(T.t2[:, 4:6], j2, CN(3), A.add)] if right is not None else []))
    MK2 = masks(2, W(G2), COL_1, G2e_)
    e = group("v", ([ts(T.t2[:, 2:4], j2, CN(2), A.add, 64.0, A.is_lt), ts(T.t2[:, 6:8], j2, CN(2), A.add, 224.0, A.add)] if left is not None else
                    [ts(T.of2[:, 2:4], j2, 0.0, A.add)]))
    wait("v", e, e1)
    o2 = []
    if right is not None:
        o2 += [ts(T.of2[:, k:k + 1], T.t2[:, k:k + 1], CN(1), A.mult, T.t2[:, 4 + k:5 + k], A.add) for k in range(2)]
    else:
        o2 += [ts(T.of2[:, 0:2], j2, 160.0, A.add)]
    if left is not None:
        o2 += [ts(T.of2[:, 2 + k:3 + k], T.t2[:, 2 + k:3 + k], K(CL64, 128), A.mult, T.t2[:, 6 + k:7 + k], A.add) for k in range(2)]
    O2 = group("v", o2)
    ev3.append(mv(3))
    M2, N2 = masks2(2, W(G2), COL_1, MK2)
    wait("s", B1, e1)
    C2 = group("s", [act(K(KR, 128), CN(1), ID, bias=K(K64, 128)), act(K(K224, 128), CN(0), ID, bias=224.0, scale=-1.0),
                     act(K(TH2, 128), CN(2), ID, bias=64.0, scale=-1.0), act(K(RR, 128), CN(3), ACT.Relu, bias=-32.0)])
    wait("s", C2)
    e = group("s", [act(K(VV_, 128), K(K224, 128), ID, bias=K(KR, 128)), act(K(TH3, 128), CN(2), ID, bias=K(K224, 128), scale=-1.0),
                    act(T.d1[:, 0:196:7], T.neg[:], ID, bias=256.0, scale=CN(3)), act(T.d1[:, 1:196:7], T.neg[:], ID, bias=64.0, scale=CN(1))])
    wait("s", e)
    e = group("s", [act(K(TH5, 128), CN(2), ID, bias=K(VV_, 128), scale=-1.0), act(T.d1[:, 3:196:7], T.neg[:], ID, bias=CN(0), scale=0.0),
                    act(T.d1[:, 4:196:7], T.neg[:], ID, bias=-192.0, scale=K(TH2, 128))])
    wait("s", e)
    TH = group("s", [act(K(TH4, 128), K(RR, 128), ID, bias=K(TH5, 128), scale=-1.0), act(K(NT5, 128), K(TH5, 128), ID, bias=-32.0),
                     act(K(COLM + 2), K(SIGM), ID, bias=T.bh[0:32, 1:2], scale=-32.0)])
    wait("s", TH, L3)
    JM = group("s", [act(T.jm[:], T.jj[:], ID, bias=K(NT5, 128), scale=-1.0)])

    def hole3():
        wait("v", *ev3)
        box["V3E"] = group("v", [qz("v3", 0, 386, T.h3)])
        wait("v", E2, O2)
        box["PC"] = group("v", [cp(T.p2[:, 0:64].bitcast(dt.uint32), T.ld2[:].bitcast(dt.uint32).indirect(T.of2[:, 0:4]))])

    def after3():
        wait("s", E2, O2)
        ps = group("s", [act(T.p2s[:, 0:64], T.ld2s[:].indirect(T.of2[:, 0:4]), ACT.Copy)])
        wait("t", GP[2], box["PC"], ps, *CS2)
        box["L3"] = late(T.pl, "p2", 0, T.h3, 0, 386, 64, "ss")
        wait("t", box["V3E"])
        my0 = group("t", [mm(T.pe, 0, "aq", 0, "v3", 0, 386)])
        wait("s", my0)
        box["Y0"] = group("s", [act(T.ysb[:, 0:386], T.pe[:, 0:386], ACT.Copy)])

    B2e, rest = border(2, CS2, MK2, M2, N2, hole3, after3)
    V3E, Y0 = box["V3E"], box["Y0"]
    wait("v", B2e, JM)
    th = [K(TH5, 128), K(TH4, 128), K(TH3, 128), K(TH2, 128), 32.0]
    e = group("v", [ts(T.d0[:, 1 + s:196:7], T.jj[:], CN(4), A.add, th[s], A.is_ge) for s in range(5)] +
              [ts(T.d0[:, 6:196:7], T.jm[:], CN(5), A.add, CN(4), A.is_gt), ts(T.d1[:, 5:196:7], T.jj[:], CN(4), A.add, 418.0, A.add)])
    wait("v", *box["L3"])
    V3L = group("v", [qz("v3", 386, 514, T.h3)])
    wait("t", V3L)
    my1 = group("t", [mm(T.pe, 1, "aq", 0, "v3", 386, 514)])
    wait("s", my1)
    Y1 = group("s", [act(T.ysb[:, 386:450], T.pe[:, 512:576], ACT.Copy)])
    wait("v", e)
    e = group("v", [lambda: V.tensor_tensor_scan(T.sc[:], T.d0[:], T.d1[:], 0.0, A.mult, A.add)])
    wait("v", e)
    O3 = group("v", [cp(T.of3[:], T.sc[:, 6:196:7])])
    H = E // 2
    half = [(H * h, H * h + H, T.of3[:, 14 * h:14 * h + 14]) for h in range(2)]
    wait("v", O3, V3E, V3L)
    wait("s", O3, Y0, Y1, V3E, V3L)
    FC, FY = [], []
    for lo, hi, off in half:
        FC.append(group("v", [cp(T.fin[:, lo:hi].bitcast(dt.uint32), T.v3[:, 0:450].bitcast(dt.uint32).indirect(off))]))
        FY.append(group("s", [act(T.yo[:, lo:hi], T.ysb[:].indirect(off), ACT.Copy)]))
        if lo == 0:
            e = group("v", rest)
        else:
            wait("v", e)
            e = columns(2)
    FS = [group("v", [cp(T.fins[:, 0:H], T.v3s[:, 0:450].indirect(half[0][2]))]),
          group("s", [act(T.fins[:, H:E], T.v3s[:, 0:450].indirect(half[1][2]), ACT.Copy)])]
    wait("v", e)
    e = group("v", [tr(T.bt[0:32, :], T.bh[0:32, :])])
    wait("v", e)
    e = group("v", [cp(T.bo[0:32, 0:N], T.bt[0:32, 0:32:4])])
    for h, (lo, hi, off) in enumerate(half):
        wait("y", FC[h])
        dma("y", [(T.oc[:, 4 * lo:4 * hi], T.fin[:, lo:hi].bitcast(dt.uint8))])
        if h == 0:
            wait("y", FY[h])
            dma("y", [(T.y[:, lo:hi], T.yo[:, lo:hi])])
    wait("s", FY[1])
    dma("s", [(T.y[:, H:E], T.yo[:, H:E])])
    wait("s", *FS)
    dma("s", [(T.osc[4 * k:4 * k + 4, :], T.fins[32 * k:32 * k + 4, :]) for k in range(2)])
    wait("y", *FS)
    dma("y", [(T.osc[4 * k:4 * k + 4, :], T.fins[32 * k:32 * k + 4, :]) for k in range(2, 4)])
    wait("s", e)
    dma("s", [(T.bd[:], T.bo[0:R, 0:N + 1])])

    g.wait_ge(T.sem.sent, sent[0])
    for name in total:
        if max(seen[q].get(name, 0) for q in Q) < total[name]:
            wait("g", (name, total[name]))
